import numpy as np, ml_dtypes
CORES = [16,17,18,19,32,33,34,35]
N = 8
import mx_ref
BF = ml_dtypes.bfloat16
def gcols(t, e):
    v = np.concatenate([t.reshape(8, 16, -1, 4), np.zeros((8, 16, 1, 4), BF)], axis=2)
    return np.ascontiguousarray(np.stack([v[g][:, e[g]] for g in range(8)])).reshape(128, -1)
def tile(rs):
    return np.stack(rs, axis=2).reshape(128, -1).astype(BF)
def pick(q, e):
    c = np.concatenate([q[0].reshape(128, -1, 4), np.zeros((128, 1, 4), np.uint8)], axis=1); s = np.concatenate([q[1], np.ones((16, 1), np.uint8)], axis=1)
    return (np.ascontiguousarray(c[:, e].reshape(128, -1)), np.ascontiguousarray(s[:, e]))
def join(*qs):
    return (np.concatenate([q[0] for q in qs], axis=1), np.concatenate([q[1] for q in qs], axis=1))
def put(q, e, v):
    c, s = q[0].reshape(128, -1, 4).copy(), q[1].copy(); c[:, e] = v[0].reshape(128, -1, 4); s[:, e] = v[1]
    return (c.reshape(128, -1), s)
def pk(c, s):
    return (np.ascontiguousarray(c), mx_ref.live(s))
def emit(q):
    return q[0], q[1]
def packed(v, rng):
    q = [mx_ref.quantize(np.ascontiguousarray(v[r])) for r in range(N)]
    return np.stack([a for a, b in q]), np.stack([mx_ref.plane(b, rng) for a, b in q])
def values_of_codes():
    e, c = np.zeros((128, 128, 4), np.float32), np.zeros((128, 2, 4), np.uint8)
    e[np.arange(128), np.arange(128), 0] = 1
    c[:127, :, 0] = np.arange(256).reshape(2, 128).T[:127]
    return mx_ref.matmul(mx_ref.quantize(e.reshape(128, 512).astype(BF)), (c.reshape(128, 8), np.full((16, 2), 127, np.uint8))).T.reshape(-1).astype(np.float64)
CODE_VALUE, SCALE_VALUE = values_of_codes(), 2.0 ** (np.arange(256) - 127.0)
def decode(q):
    return (CODE_VALUE[q[0]].reshape(16, 8, -1, 4) * SCALE_VALUE[q[1]][:, None, :, None] + 0.0).reshape(128, -1).astype(np.float32)
def f(rng, *shape):
    return mx_ref.flush((rng.standard_normal(shape, dtype=np.float32) * np.exp2(rng.integers(-2, 3, shape[:-1] + (1,)))).astype(BF))
def wide(rng, *shape, cols=0):
    v = rng.standard_normal(shape, dtype=np.float32) * np.exp2(rng.integers(-12, 13, shape)).astype(np.float32)
    if cols: v *= np.repeat(np.exp2(rng.integers(-cols, cols + 1, shape[:-2] + (1, shape[-1] // 4))) * (rng.random(shape[:-2] + (1, shape[-1] // 4)) > 0.0625), 4, axis=-1).astype(np.float32)
    return mx_ref.flush(v.astype(BF))
C, R = 320, 3
STEP = [1, 2, 4]
def units(s, way):
    p = s[::16] + np.float32(0.0)
    n = 1 + (s[1::16] > 0) + (s[2::16] > 0) + (s[3::16] > 0)
    o = np.argsort(np.float32(way) * p, axis=1, kind="stable")
    return [np.repeat(o[g], n[g][o[g]]) for g in range(8)]
def segments(bids, asks):
    e, first = np.zeros((2, 8, C), np.int64), np.full((2, 8, C), -1)
    for g in range(8):
        m = min(len(bids[g]), len(asks[g]))
        a = np.stack([bids[g][:m], asks[g][:m]])
        new = np.concatenate([[True], (a[:, 1:] != a[:, :-1]).any(axis=0)])
        e[:, g] = a[:, np.flatnonzero(new)[:C]]
        for i in range(2):
            c, k = np.unique(e[i, g], return_index=True)
            first[i, g, c] = k
    return e, first
def numbers_of(rng):
    return {"x": np.array(f(rng, N, 128, 4 * C)), "u": np.stack([f(rng, 128, 512)] * N), "v": np.array(f(rng, N, 128, 512))}
def common(w, rng):
    c, p = packed(np.stack([w] * N), rng)
    return {"wc": c, "ws": p}
def planted(rng, s, n, less=()):
    d = numbers_of(rng)
    kind = rng.permutation(8) % 3
    sign = np.stack([rng.permutation(8) % 2 * 2.0 - 1.0 for r in range(N)])
    k = np.where(kind > 0, 2.0 ** -30, 1.0)
    x = d["x"].astype(np.float32).reshape(N, 8, 16, C, 4)
    e = ((s[..., None] >> np.arange(8)) & 1) * np.exp2(np.arange(8) - 23.0)
    e = e * np.where(kind == 2, sign * 2.0 ** -7, 1.0)[:, :, None, None] + 0.0
    one = np.repeat(np.where(kind < 2, sign, 0.0)[:, :, None], C, axis=2)
    for r in range(N):
        for g in rng.permutation(8)[:4]: one[r, g, rng.integers(C)] = sign[r, g] * 2.0 ** 30
    price = one + np.sum(e, axis=3)
    for r, g in less:
        n[r, g, np.argmin(price[r, g]) if r % 2 else np.argmax(price[r, g])] = 2
    q = np.where(np.argsort(rng.random((N, 8, C, 3)), axis=3) < n[..., None] - 1, 1, -rng.integers(0, 2, (N, 8, C, 3)))
    x[:, :, 0] = 0
    x[:, :, 0, :, 0] = one
    x[:, :, 8] = e[..., :4]
    x[:, :, 9] = e[..., 4:]
    x[:, :, 10] = 0
    x[:, :, 10, :, :3] = q * np.where(kind == 2, 2.0 ** -30, 2.0 ** -20)[:, None, None]
    x[:, :, 11:] = rng.integers(4, 8, (N, 8, 5, C, 4)) * rng.choice([-1.0, 1.0], (N, 8, 5, C, 4)) * 2.0 ** -20
    u = d["u"][0].astype(np.float32).reshape(128, 128, 4)
    for g in range(8):
        h = 16 * g
        u[:, h:h + 4] = 0
        u[h, h, 0] = k[g]
        u[h + 8:h + 10, h] = k[g]
        for i in range(3): u[h + 10, h + 1 + i, i] = k[g]
    w = np.array(f(rng, 128, 2048)).reshape(128, 4, 8, 16, 4)
    w[::16] = 0
    w[:, :, :, 0] = 0
    w[:, :, :, 8:] = 0
    return {"x": x.reshape(N, 128, 4 * C).astype(BF), "u": np.stack([u.reshape(128, 512).astype(BF)] * N), "v": d["v"], **common(w.reshape(128, 2048), rng)}
def pairs_of(rng):
    return np.argsort(rng.random((N, 8, C)), axis=2) // 2
def setup_inputs(rng):
    return {**numbers_of(rng), **common(f(rng, 128, 2048), rng)}
def setup_inputs_ties(rng):
    d = numbers_of(rng)
    o = rng.permutation(N)
    x = d["x"].reshape(N, 8, 16, C, 4)
    for r in range(N):
        k = np.zeros(C, int) if r == o[0] else rng.permutation(C) % 3
        a = x[r][:, :8, :3].copy()
        a[:, :, 2] = 0
        x[r][:, :8] = a[:, :, k]
    x[o[1]] = 0
    u = d["u"].reshape(N, 8, 16, 128, 4)
    u[:, :, 8:, ::16] = 0
    w = np.array(f(rng, 128, 2048)).reshape(128, 4, 8, 16, 4)
    w[:, :, :, :8] = 0
    return {"x": x.reshape(N, 128, 4 * C), "u": u.reshape(N, 128, 512), "v": d["v"], **common(w.reshape(128, 2048), rng)}
def setup_inputs_near(rng):
    return planted(rng, pairs_of(rng), rng.integers(1, 5, (N, 8, C)))
def setup_inputs_lots(rng):
    n = np.zeros((N, 8, C), np.int64)
    p = rng.permutation(N // 2)
    h = rng.permutation(8) % 2
    less = []
    for i in range(N // 2):
        c = (p[i] + N // 2 * h) % 4
        k = np.array([(1, 4), (2, 3), (4, 4), (1, 1)])[c]
        j = int(rng.integers(2))
        n[2 * i], n[2 * i + 1] = k[:, j, None], k[:, 1 - j, None]
        g = rng.permutation(np.flatnonzero(c == 2))
        less += [(2 * i, int(a)) for a in g[::4]] + [(2 * i + 1, int(a)) for a in g[1::4]]
    return planted(rng, pairs_of(rng), n, less)
def setup_inputs_huge(rng):
    d = numbers_of(rng)
    x = 2.0 ** 30 * (0.6 + 0.2 * rng.random((N, 128, C, 4)))
    c = np.stack([rng.permutation(C) % 2 * 2.0 - 1.0 for r in range(N)])
    o = rng.permutation(N)
    c[o < N // 2] = 1
    c[o == 0] = -1
    x *= c[:, None, :, None]
    u = d["u"][0].astype(np.float32).reshape(128, 128, 4)
    u[:, ::16] = 2.0 ** 30 * (1 - 0.25 * rng.random((128, 8, 4))) * (rng.permutation(8) % 2 * 2.0 - 1.0)[None, :, None]
    w = np.zeros((128, 4, 128, 4), np.float32)
    i = np.arange(128)
    for b in range(4): w[i, b, i, b] = 1
    return {"x": x.astype(np.float32).reshape(N, 128, 4 * C).astype(BF), "u": np.stack([u.reshape(128, 512).astype(BF)] * N), "v": d["v"], **common(w.reshape(128, 2048).astype(BF), rng)}
def setup_inputs_spread(rng):
    d = setup_inputs(rng)
    d["x"] = wide(rng, N, 128, 4 * C, cols=6)
    return d
def check_inputs(d):
    b = []
    for k in ("x", "u", "v"):
        a = np.abs(d[k].astype(np.float32))
        if not (np.isfinite(a).all() and ((a == 0) | (a >= 2.0 ** -30) & (a <= 2.0 ** 30)).all()): b.append("a value of " + k)
    a = d["u"].astype(np.float32)
    if (a != a[:1]).any(): b.append("u differs between ranks")
    if (d["wc"] != d["wc"][:1]).any(): b.append("wc differs between ranks")
    s = [mx_ref.live(p) for p in d["ws"]]
    if any((p != s[0]).any() for p in s): b.append("ws differs between ranks")
    return b
def reference(x, u, v, wc, ws):
    w = pk(wc[0], ws[0])
    lay = [pick(w, np.arange(128 * b, 128 * b + 128)) for b in range(4)]
    qu = mx_ref.quantize(u[0])
    now = [x[r] for r in range(N)]
    lists = [None] * N
    for t in range(R):
        held, score = [], []
        for r in range(N):
            q = mx_ref.quantize(now[r])
            held.append(decode(q).astype(BF))
            score.append(mx_ref.matmul(qu, q))
        for r in range(N):
            s = r ^ STEP[t]
            if s < r: continue
            e, first = segments(units(score[r], -1), units(score[s], 1))
            z = gcols(held[r], e[0]).astype(np.float32) + gcols(held[s], e[1]).astype(np.float32)
            q = mx_ref.quantize((z * np.float32(0.5)).astype(BF))
            h = tile([np.maximum(mx_ref.matmul(lay[b], q), np.float32(0.0)) * np.float32(0.03125) for b in range(4)])
            h = decode(mx_ref.quantize(h)).astype(BF)
            for i, k in ((0, r), (1, s)):
                now[k] = (held[k].astype(np.float32) + gcols(h, first[i]).astype(np.float32)).astype(BF)
                lists[k] = first[i]
    y, ol = np.zeros((N, 128, C), np.float32), np.zeros((N, 8, C), np.float32)
    oc, osc = np.zeros((N, 128, 4 * C), np.uint8), np.zeros((N, 16, C), np.uint8)
    for r in range(N):
        q = mx_ref.quantize(now[r])
        y[r] = mx_ref.matmul(mx_ref.quantize(v[r]), q)
        ol[r] = lists[r]
        oc[r], osc[r] = emit(q)
    return {"y": y, "ol": ol, "oc": oc, "osc": osc}

@@ -1,0 +1,445 @@
+import numpy as np
+from concourse.mybir import dt, AluOpType, ActivationFunctionType
+
+C, R, STEP = 320, 3, [1, 2, 4]
+ZC, XC = 192, 160
+HW = 336
+Q4, U8, BF, F32, I32, U16, F16 = "float8_e4m3fn_x4", "uint8", "bfloat16", "float32", "int32", "uint16", "float16"
+OWN, FAR = [4, 5, 6, 0], [1, 2, 3, 7]
+SUM = [7, 3]
+SPLIT = [[3], [2, 3]]
+TURN = [3, 2, 1, 0, 4, 5, 6, 7, 9, 8]
+
+SCRATCH = {}
+
+
+def _sb(name, n, d):
+    SCRATCH[name] = ("sbuf", [128, n], d)
+
+
+def _pair(name, n):
+    _sb(name + "q", n, Q4)
+    _sb(name + "s", n, U8)
+
+
+for _n, _w, _d in [
+        ("x0", 1280, BF), ("xs", 1280, BF), ("ut", 512, BF), ("vt", 512, BF), ("et", 2048, BF), ("st", 512, BF),
+        ("ones", 512, BF), ("ioff", 16, I32), ("uoff", 16, U16), ("pc", 8, I32), ("pm", 8, I32), ("pf", 8, F32),
+        ("r16", C, BF), ("r32", 64, BF), ("tri", 64, BF), ("cq", C, BF), ("alt", 2 * C, BF), ("wi", 20, F32),
+        ("wu", 40, F32), ("mask", C, BF), ("keep", C, BF), ("cbig", C, BF), ("keyj", C, F32), ("half", C, BF),
+        ("tp", C, F32), ("qa", C, BF), ("qq", C, BF), ("sg", 20 * C, BF), ("ft", 5 * 1280, BF),
+        ("m1", C, F16), ("m2", C, F16), ("mk16", C, F16), ("kp16", C, F16), ("key", C, F32),
+        ("un", 1280, BF), ("sn", 1280, BF), ("m3", C, BF), ("m4", C, BF), ("ta", 40, F32), ("td", 40, F32),
+        ("os_", 20, U16), ("of_", 20, U16), ("vw", 640, F32), ("y1", C, F32), ("y2", C, F32),
+        ("ki", 20, I32), ("kj", 20, I32), ("do_", 1280, BF), ("dp", 1280, BF), ("df", 1280, BF),
+        ("zo", 1280, BF), ("zi", 1280, BF), ("z", 1280, BF), ("hs", 4 * HW, BF), ("hp", 1280, BF),
+        ("fr", C, F32), ("fm", C, F32), ("fo", C, F32), ("yo", C, F32)]:
+    _sb(_n, _w, _d)
+for _n, _w in [("u", 128), ("up", 256), ("v", 128), ("w", 512), ("e", 512), ("s", 128), ("f", 5 * C), ("z", C), ("h", C)]:
+    _pair("c" + _n, _w)
+for _t in range(R + 1):
+    _pair("t%d" % _t, C)
+for _t in range(R):
+    _pair("l%d" % _t, C)
+    for _n in ("lo", "la", "li", "lb"):
+        _sb("%s%d" % (_n, _t), 20, U16)
+SCRATCH["ps"] = ("psum", [128, 4096], F32)
+
+SEMAPHORES = (["cV", "cA", "cT", "cG", "sent", "dx0", "dx1", "du", "dv", "dw", "out"]
+              + ["%s%d" % (n, t) for t in range(R) for n in ("aT", "aA", "aB")])
+
+
+def rank_program(g, core, T, topo):
+    rank = T.rank_of(core)
+    if rank is None:
+        return
+    A = AluOpType
+    F = ActivationFunctionType
+    queue = {"V": g.vector, "A": g.scalar, "T": g.tensor, "G": g, "S": g.sync}
+    own = {"V": "cV", "A": "cA", "T": "cT", "G": "cG"}
+    count = {}
+    clock = {k: {} for k in queue}
+    events = []
+    wrote, read = {}, {}
+
+    def view(name, a=0, b=None, s=1, p=None):
+        n = SCRATCH[name][1][1]
+        b = n if b is None else b
+        rows = slice(0, 128) if p is None else slice(p[0], p[1])
+        ap = T[name][rows, a:b] if s == 1 else T[name][rows, a:b:s]
+        if name == "ps":
+            return (ap, [(name, np.arange(a // 512, a // 512 + 1))])
+        return (ap, [(name, np.arange(a, b, s))])
+
+    def bank(k, n=C, a=0):
+        return view("ps", 512 * k + a, 512 * k + n)
+
+    def by(win, off):
+        return (win[0].indirect(off[0]), win[1] + off[1])
+
+    def cast(x, d):
+        return (x[0].bitcast(d), x[1])
+
+    def marks(table, name):
+        if name not in table:
+            n = 8 if name == "ps" else SCRATCH[name][1][1]
+            table[name] = {k: np.full(n, -1) for k in list(queue) + ["X"]}
+        return table[name]
+
+    def wait(q, sem, val, snap):
+        if clock[q].get(sem, 0) < val:
+            queue[q].wait_ge(T.sem[sem], int(val))
+            clock[q][sem] = val
+        for k in snap:
+            if clock[q].get(k, 0) < snap[k]:
+                clock[q][k] = snap[k]
+
+    def order(q, outs, ins, adds=False):
+        need = set()
+        for x in ins:
+            for name, idx in x[1]:
+                for k, m in marks(wrote, name).items():
+                    need.update(m[idx].tolist())
+                if name == "ps":
+                    for k, m in marks(read, name).items():
+                        if k != q:
+                            need.update(m[idx].tolist())
+        for x in outs:
+            for name, idx in x[1]:
+                for table in (wrote, read):
+                    for k, m in marks(table, name).items():
+                        if not (adds and k == q):
+                            need.update(m[idx].tolist())
+        need.discard(-1)
+        for e in sorted(need, reverse=True):
+            wait(q, events[e][0], events[e][1], events[e][3])
+
+    def note(q, sem, n, outs, ins):
+        count[sem] = count.get(sem, 0) + n
+        events.append((sem, count[sem], q, dict(clock[q]) if q != "X" else {}))
+        for table, xs in ((read, ins), (wrote, outs)):
+            for x in xs:
+                for name, idx in x[1]:
+                    marks(table, name)[q][idx] = len(events) - 1
+
+    def run(q, call, outs, ins, adds=False):
+        order(q, outs, ins, adds)
+        call().then_inc(T.sem[own[q]], 1)
+        note(q, own[q], 1, outs, ins)
+
+    def isview(x):
+        return isinstance(x, tuple)
+
+    def copy(out, in_):
+        run("V", lambda: g.vector.tensor_copy(out[0], in_[0]), [out], [in_])
+
+    def scatter(win, off, vals):
+        run("V", lambda: g.vector.tensor_copy(win[0].indirect(off[0]), vals[0]), [win], [off, vals])
+
+    def tt(out, a, b, op):
+        run("V", lambda: g.vector.tensor_tensor(out[0], a[0], b[0], op), [out], [a, b])
+
+    def ts(out, a, s1, op0, s2=None, op1=None):
+        ins = [a] + [s for s in (s1, s2) if isview(s)]
+        x1, x2 = (s1[0] if isview(s1) else s1), (s2[0] if isview(s2) else s2)
+        if op1 is None:
+            run("V", lambda: g.vector.tensor_scalar(out[0], a[0], x1, None, op0), [out], ins)
+        else:
+            run("V", lambda: g.vector.tensor_scalar(out[0], a[0], x1, x2, op0, op1), [out], ins)
+
+    def scan(out, d0, d1, init, op0, op1):
+        run("V", lambda: g.vector.tensor_tensor_scan(out[0], d0[0], d1[0], init, op0, op1), [out], [d0, d1])
+
+    def fill(out, c):
+        run("V", lambda: g.vector.memset(out[0], c), [out], [])
+
+    def act(out, in_, func, bias=None, scale=None):
+        kw = {}
+        if bias is not None:
+            kw["bias"] = bias[0] if isview(bias) else bias
+        if scale is not None:
+            kw["scale"] = scale
+        run("A", lambda: g.scalar.activation(out[0], in_[0], func, **kw), [out], [in_] + ([bias] if isview(bias) else []))
+
+    def move(on_vector, out, in_):
+        if on_vector:
+            copy(out, in_)
+        else:
+            act(out, in_, F.Copy)
+
+    def pair(name, a=0, b=None):
+        return (view(name + "q", a, b), view(name + "s", a, b))
+
+    def quant(p, tile):
+        run("V", lambda: g.vector.quantize_mx(p[0][0], p[1][0], tile[0]), [p[0], p[1]], [tile])
+
+    def mm(out, w, x, start=True, stop=True):
+        run("T", lambda: g.tensor.matmul_mx(out[0], w[0][0], w[1][0], x[0][0], x[1][0], start, stop),
+            [out], [w[0], w[1], x[0], x[1]], adds=not start)
+
+    def iota(out, pattern, base, mult):
+        if SCRATCH[out[1][0][0]][2] == I32:
+            run("G", lambda: g.iota(out[0], pattern, base, mult), [out], [])
+        else:
+            run("G", lambda: g.iota(out[0], pattern, base, mult, allow_small_or_imprecise_dtypes=True), [out], [])
+
+    def load(q, sem, jobs):
+        for out, src in jobs:
+            queue[q].dma_start(out[0], src).then_inc(T.sem[sem], 16)
+        note(q, sem, 16 * len(jobs), [j[0] for j in jobs], [])
+
+    def store(q, dst, src):
+        order(q, [], [src])
+        queue[q].dma_start(dst, src[0]).then_inc(T.sem.out, 16)
+        count["out"] = count.get("out", 0) + 16
+
+    def send(peer, sem, jobs):
+        rid, pid, _ = topo.addr(peer)
+        n = len(topo.engines(core, peer))
+        for dst, src in jobs:
+            order("G", [], [src])
+            g.remote_dma(dst[0], src[0], T.sem[sem], T.sem.sent, pid, rid, topo.mask(core, peer))
+            count["sent"] = count.get("sent", 0) + n
+        note("X", sem, len(topo.engines(peer, core)) * len(jobs), [j[0] for j in jobs], [])
+
+    XP, ZP, SP = [(0, XC), (XC, C)], [(0, ZC), (ZC, C)], [(0, C // 2), (C // 2, C)]
+    load("A", "du", [(view("ut"), T.u[:])])
+    for i, (a, b) in enumerate(XP):
+        load("S", "dx%d" % i, [(view("x0", 4 * a, 4 * b), T.x[:, 4 * a:4 * b])])
+    iota(view("ioff"), [[16, 2], [32, 4], [0, 2]], 0, 0)
+    iota(view("pc", 0, 1), [[1, 1]], 0, 1)
+    iota(view("r32"), [[1, 32], [0, 2]], 0, 0)
+    iota(view("r16"), [[0, 20], [1, 16]], 0, 0)
+    iota(view("wi"), [[16, 20]], 0, 0)
+    fill(view("ones"), 1.0)
+    fill(view("st"), 0.0)
+    copy(view("uoff"), view("ioff"))
+    ts(view("pm", 0, 1), view("pc", 0, 1), 15, A.bitwise_and)
+    ts(view("pm", 1, 2), view("pc", 0, 1), 31, A.bitwise_and)
+    for a in range(4):
+        for h in range(2):
+            o = 4 * (32 * a + 16 * h) + h
+            fill(view("st", o, o + 64 - h, 2, (32 * a, 32 * a + 32)), 512.0)
+    copy(view("pf", 0, 2), view("pm", 0, 2))
+    fill(view("cq"), 8.0)
+    quant(pair("cs"), view("st"))
+    ts(view("tri"), view("r32"), view("pf", 1, 2), A.is_gt, 0.5, A.subtract)
+    fill(view("cq", 1, C, 16), 1.0)
+    fill(view("half"), 0.5)
+    fill(view("wu"), 0.0)
+    fill(view("alt"), 1.0)
+    fill(view("hs", C, 4 * HW, HW), 0.0)
+    ts(view("mk16"), view("r16"), view("pf", 0, 1), A.is_equal, 1.0 / 512, A.mult)
+    ts(view("kp16"), view("r16"), 1.0, A.min)
+    for name, n in (("un", 1280), ("vw", C)):
+        for a in range(0, n, 512):
+            act(view(name, a, min(n, a + 512)), view("ones", 0, min(n, a + 512) - a), F.Copy, None, 0.0)
+
+    def later():
+        ts(view("mask"), view("r16"), view("pf", 0, 1), A.is_equal)
+        ts(view("cbig"), view("r16"), view("pf", 0, 1), A.is_equal, 2.0 ** 21, A.mult)
+        ts(view("keep"), view("r16"), 1.0, A.min)
+        ts(view("wu", 1, 40, 2), view("wi"), view("pf", 0, 1), A.add)
+        fill(view("alt", 0, 2 * C, 2), 0.0)
+
+    def unit(b):
+        out, src = view("et", 512 * b, 512 * b + 512), view("ones")
+        run("G", lambda: g.affine_select(out[0], src[0], [[1, 512]], A.is_equal, 0.0, -b, -4), [out], [src])
+
+    unit(0)
+    unit(1)
+    quant(pair("cu"), view("ut"))
+    copy(cast(view("cupq"), dt.uint32), by(cast(view("cuq"), dt.uint32), view("uoff")))
+    act(view("cups"), by(view("cus"), view("uoff")), F.Copy)
+    for a, b in XP:
+        quant(pair("t0", a, b), view("x0", 4 * a, 4 * b))
+    order("S", [], [view("x0")])
+    load("S", "dw", [(cast(view("cwq"), dt.uint8), T.wc[:]), (view("cws"), T.ws[:])])
+    load("S", "dv", [(view("vt"), T.v[:])])
+
+    E = [pair("ce", 128 * b, 128 * b + 128) for b in range(4)]
+    W = [pair("cw", 128 * b, 128 * b + 128) for b in range(4)]
+
+    for t in range(R):
+        mate = rank ^ STEP[t]
+        peer = T.cores[mate]
+        buys = rank < mate
+        mine, theirs = "t%d" % t, "l%d" % t
+        lo, la, li, lb = [view("%s%d" % (n, t)) for n in ("lo", "la", "li", "lb")]
+        first = C if topo.chip(core) == topo.chip(peer) else XC
+
+        def hand(a, b):
+            send(peer, "aT%d" % t, [(cast(view(theirs + "q", a, b), dt.uint8), cast(view(mine + "q", a, b), dt.uint8)),
+                                    (view(theirs + "s", a, b), view(mine + "s", a, b))])
+
+        mm(bank(0, XC), pair("cu"), pair(mine, 0, XC))
+        mm(bank(3, C - XC), pair("cu"), pair(mine, XC, C))
+        mm(bank(1), pair("cup", 0, 128), pair(mine))
+        mm(bank(2), pair("cup", 128, 256), pair(mine))
+        hand(0, first)
+        for i, (a, b) in enumerate(XP):
+            src, dst = bank(3 * i, b - a), view("tp", a, b)
+            run("V", lambda: g.vector.transpose(dst[0], src[0]), [dst], [src])
+            ts(view("qa", a, b), dst, 0.0, A.is_gt)
+            scan(view("qq", a, b), view("cq", a, b), view("qa", a, b), 1.0, A.min, A.add)
+        if t == 0:
+            unit(2)
+            unit(3)
+            iota(view("keyj"), [[1, C]], 512, 0)
+        else:
+            for b in range(4):
+                mm(bank(OWN[b]), E[b], pair(mine))
+        cmp_, tie, loose = (A.is_gt, A.add, -0.5) if buys else (A.is_lt, A.subtract, 0.5)
+
+        def total(w):
+            final = w == TURN[-1] // 2
+            for a, b in (SP if final else [(0, C)]):
+                quant(pair("cf", C * w + a, C * w + b), view("ft", 1280 * w + 4 * a, 1280 * w + 4 * b))
+            for i, (a, b) in enumerate(SP):
+                mm(bank(SUM[i], b - a), pair("cs"), pair("cf", C * w + a, C * w + b), w == TURN[0] // 2, final)
+
+        def earlier(m, a0, a1, lim):
+            s0, f0 = 2 * C * (m // 2) + m % 2, 1280 * (m // 4) + m % 4
+            if a1 > a0:
+                ts(view("ft", f0 + 4 * a0, f0 + 4 * a1 - 3, 4), view("sg", s0 + 2 * a0, s0 + 2 * a1 - 1, 2), lim, cmp_,
+                   view("qq", 16 * m + 3, 16 * m + 4), A.mult)
+
+        for n, b in enumerate(TURN):
+            cut = 0 if b == 0 else (32 * b + 32 if b < 5 or b == 9 else 32 * b)
+            parts = [(cut, C, loose), (0, cut, 0.0)]
+            if cut == 32 * b:
+                parts.reverse()
+            s0 = 2 * C * b
+            for h in range(2):
+                m = 2 * b + h
+                act(view("sg", s0 + h, s0 + 2 * C, 2), bank(1 + h), F.Sign, view("tp", 16 * m, 16 * m + 1), -1.0)
+                if h:
+                    d = view("sg", s0 + 64 * b, s0 + 64 * b + 64)
+                    tt(d, d, view("tri"), tie)
+                earlier(m, *parts[0])
+            if n % 2 == 0 and n:
+                total(TURN[n - 1] // 2)
+            for h in range(2):
+                earlier(2 * b + h, *parts[1])
+        total(TURN[-1] // 2)
+        for i, (a, b) in enumerate(SP):
+            tt(view("m1", a, b), bank(SUM[i], b - a), view("mk16", a, b), A.mult)
+        scan(view("m2"), view("kp16"), view("m1"), 0.0, A.mult, A.add)
+        copy(lo, view("m2", 15, C, 16))
+        send(peer, "aA%d" % t, [(la, lo)])
+        if first < C:
+            hand(first, C)
+
+        if t == 0:
+            quant(pair("ce"), view("et"))
+            for b in range(4):
+                mm(bank(OWN[b]), E[b], pair(mine))
+        for i, (a, b) in enumerate(SP):
+            tt(view("key", a, b), bank(SUM[i], b - a), view("keyj", a, b), A.add)
+        scatter(view("un"), lo, view("half"))
+        if t == 0:
+            later()
+        for b in range(4):
+            mm(bank(FAR[b]), E[b], pair(theirs))
+        for b in range(4):
+            act(view("do_", C * b, C * b + C), bank(OWN[b]), F.Copy, None, 0.5)
+            act(view("df", C * b + XC, C * b + C), bank(OWN[b], C, XC), F.Copy)
+        for b in range(4):
+            act(view("dp", C * b, C * b + C), bank(FAR[b]), F.Copy, None, 0.5)
+
+        scatter(view("un"), la, view("half"))
+        scan(view("sn"), view("un"), view("un"), -161.0, A.add, A.add)
+        tt(view("m3"), by(view("sn"), lo), view("mask"), A.mult)
+        scan(view("m4"), view("keep"), view("m3"), 0.0, A.mult, A.add)
+        seg = view("m4", 15, C, 16)
+        ts(view("ta", 0, 40, 2), seg, 160.0, A.is_ge, 1024.0, A.mult)
+        ts(view("ta", 1, 40, 2), seg, 160.0, A.add, float(C), A.min)
+        scan(view("td"), view("wu"), view("ta"), 0.0, A.min, A.add)
+        copy(view("os_"), view("td", 1, 40, 2))
+        scatter(view("vw"), view("os_"), view("key"))
+        scan(view("y1"), view("vw", 0, C), view("vw", 0, C), 0.0, A.max, A.max)
+        scan(view("y2"), view("cbig"), view("y1"), 0.0, A.max, A.min)
+        copy(view("ki"), view("y2", 15, C, 16))
+        ts(view("kj"), view("ki"), 511, A.bitwise_and)
+        copy(li, view("kj"))
+        send(peer, "aB%d" % t, [(lb, li)])
+
+        if t + 1 < R:
+            iota(view("un"), [[0, 1280]], 0, 0)
+            iota(view("vw", 0, C), [[0, C]], 0, 0)
+        for b in range(4):
+            for a0, a1 in ([(0, C)] if b < 2 else ZP):
+                if b in SPLIT[a0 > 0]:
+                    out = view("zi", 2 * C * (b - 2) + 2 * a0, 2 * C * (b - 2) + 2 * a1, 2)
+                else:
+                    out = view("zo", C * b + a0, C * b + a1)
+                move(b >= 2, out, by(view("do_", C * b, C * b + C), view("li%d" % t, a0 // 16, a1 // 16)))
+        copy(view("of_"), view("ta", 1, 40, 2))
+        if t == 0:
+            quant(pair("cv"), view("vt"))
+        if t + 1 == R:
+            act(view("fr"), by(view("sn"), lo), F.Identity, 161.0)
+            ts(view("fm"), view("fr"), C + 0.5, A.is_lt)
+            tt(view("fo"), view("fr"), view("fm"), A.mult)
+            ts(view("fo"), view("fo"), -1.0, A.add)
+            for k in range(8):
+                store("S", T.ol[k:k + 1, :], view("fo", 0, C, 1, (16 * k, 16 * k + 1)))
+
+        def far(b, a0, a1):
+            return by(view("dp", C * b, C * b + C), view("lb%d" % t, a0 // 16, a1 // 16))
+
+        for i, (a0, a1) in enumerate(ZP):
+            for b in SPLIT[i]:
+                o = 2 * C * (b - 2)
+                act(view("zi", o + 2 * a0 + 1, o + 2 * a1, 2), far(b, a0, a1), F.Copy)
+        for i, (a0, a1) in enumerate(ZP):
+            for b in ([0, 2, 3, 1] if i == 0 else [2, 3, 0, 1]):
+                if b in SPLIT[i]:
+                    o = 2 * C * (b - 2)
+                    scan(view("z", 4 * a0 + b - 2, 4 * a1, 2), view("alt", 2 * a0, 2 * a1),
+                         view("zi", o + 2 * a0, o + 2 * a1), 0.0, A.mult, A.add)
+                else:
+                    tt(view("z", 4 * a0 + b, 4 * a1, 4), far(b, a0, a1), view("zo", C * b + a0, C * b + a1), A.add)
+            quant(pair("cz", a0, a1), view("z", 4 * a0, 4 * a1))
+            for b in range(4):
+                mm(bank(4 * i + b, a1 - a0), W[b], pair("cz", a0, a1))
+        for i, (a0, a1) in enumerate(ZP):
+            for b in range(4):
+                out = view("hs", HW * b + a0, HW * b + a1)
+                if i and b == 0:
+                    ts(out, bank(4 * i + b, a1 - a0), 0.0, A.max, 0.03125, A.mult)
+                else:
+                    act(out, bank(4 * i + b, a1 - a0), F.Relu, None, 0.03125)
+
+        nxt = "t%d" % (t + 1)
+        for b in range(4):
+            mm(bank(b, XC), E[b], pair(mine, 0, XC), True, False)
+        for i, (a0, a1) in enumerate(XP):
+            for j, b in ([(0, 0), (0, 1), (0, 2), (0, 3), (1, 0)] if i == 0 else [(1, 1), (1, 2), (1, 3)]):
+                move(b % 2 == 0, view("hp", 4 * XP[j][0] + b, 4 * XP[j][1], 4),
+                     by(view("hs", HW * b, HW * b + HW), view("of_", XP[j][0] // 16, XP[j][1] // 16)))
+            quant(pair("ch", a0, a1), view("hp", 4 * a0, 4 * a1))
+            for b in range(4):
+                mm(bank(4 * i + b, a1 - a0), E[b], pair("ch", a0, a1), i == 1, True)
+        for b in range(4):
+            act(view("xs", b, 4 * XC, 4), bank(b, XC), F.Copy)
+        for b in range(4):
+            tt(view("xs", 4 * XC + b, 4 * C, 4), bank(4 + b, C - XC), view("df", C * b + XC, C * b + C), A.add)
+            if b == 0:
+                quant(pair(nxt, 0, XC), view("xs", 0, 4 * XC))
+        quant(pair(nxt, XC, C), view("xs", 4 * XC, 4 * C))
+
+    last = "t%d" % R
+    for i, (a0, a1) in enumerate(XP):
+        mm(bank(i, a1 - a0), pair("cv"), pair(last, a0, a1))
+        store("S", T.oc[:, 4 * a0:4 * a1], cast(view(last + "q", a0, a1), dt.uint8))
+    act(view("yo", 0, XC), bank(0, XC), F.Copy)
+    store("A", T.y[:, 0:XC], view("yo", 0, XC))
+    copy(view("yo", XC, C), bank(1, C - XC))
+    for k in range(4):
+        store("A", T.osc[4 * k:4 * k + 4, :], view(last + "s", 0, C, 1, (32 * k, 32 * k + 4)))
+    store("S", T.y[:, XC:C], view("yo", XC, C))
+    g.sync.wait_ge(T.sem.out, count["out"])
+    g.wait_ge(T.sem.sent, count["sent"])
+    for sem in ("cV", "cA", "cT", "cG"):
+        g.wait_ge(T.sem[sem], count[sem])

@@ -2,13 +2,21 @@ import numpy as np
 from concourse.mybir import dt, AluOpType, ActivationFunctionType
 
 C, R, STEP = 320, 3, [1, 2, 4]
-ZC, XC = 192, 160
+ZC, XC = 160, 160
+TC = 192
 HW = 336
 Q4, U8, BF, F32, I32, U16, F16 = "float8_e4m3fn_x4", "uint8", "bfloat16", "float32", "int32", "uint16", "float16"
-OWN, FAR = [4, 5, 6, 0], [1, 2, 3, 7]
-SUM = [7, 3]
+ROW, SCO, SUM = [1, 2], [0, 3], [7, 3]
+OWN, FAR = [4, 5, 6, 0], [1, 2, 7, 3]
 SPLIT = [[3], [2, 3]]
-TURN = [3, 2, 1, 0, 4, 5, 6, 7, 9, 8]
+TURN = [2, 3, 1, 0, 4, 5, 6, 7, 8, 9]
+HEAD = 3
+LC, LATE = 128, [6, 7, 8, 9]
+JOINT = [(0, 0), (0, 2), (0, 3), (1, 2), (0, 1), (1, 3), (0, None), (1, 0), (1, 1), (1, None)]
+AFTER = [("A", "r", 0, 0), ("A", "r", 0, 1), ("A", "r", 0, 2), ("A", "r", 0, 3), ("V", "r", 1, 0), ("A", "r", 1, 1),
+         ("V", "g", 0, 0), ("A", "r", 1, 2), ("V", "g", 0, 1), ("A", "r", 1, 3), ("A", "g", 0, 2), ("V", "g", 0, 3),
+         ("A", "g", 1, 0), ("V", "q", 0, 0), ("A", "g", 1, 1), ("V", "g", 1, 2), ("V", "g", 1, 3), ("V", "q", 1, 0)]
+ACC = [[0, 1], [0, 2]]
 
 SCRATCH = {}
 
@@ -24,18 +32,18 @@ def _pair(name, n):
 
 for _n, _w, _d in [
         ("x0", 1280, BF), ("xs", 1280, BF), ("ut", 512, BF), ("vt", 512, BF), ("et", 2048, BF), ("st", 512, BF),
-        ("ones", 512, BF), ("ioff", 16, I32), ("uoff", 16, U16), ("pc", 8, I32), ("pm", 8, I32), ("pf", 8, F32),
-        ("r16", C, BF), ("r32", 64, BF), ("tri", 64, BF), ("cq", C, BF), ("alt", 2 * C, BF), ("wi", 20, F32),
-        ("wu", 40, F32), ("mask", C, BF), ("keep", C, BF), ("cbig", C, BF), ("keyj", C, F32), ("half", C, BF),
-        ("tp", C, F32), ("qa", C, BF), ("qq", C, BF), ("sg", 20 * C, BF), ("ft", 5 * 1280, BF),
-        ("m1", C, F16), ("m2", C, F16), ("mk16", C, F16), ("kp16", C, F16), ("key", C, F32),
-        ("un", 1280, BF), ("sn", 1280, BF), ("m3", C, BF), ("m4", C, BF), ("ta", 40, F32), ("td", 40, F32),
-        ("os_", 20, U16), ("of_", 20, U16), ("vw", 640, F32), ("y1", C, F32), ("y2", C, F32),
+        ("ones", 512, BF), ("eye", 128, BF), ("ioff", 24, F32), ("uoff", 24, U16), ("pc", 8, I32), ("pm", 8, I32),
+        ("pf", 8, F32), ("r16", 336, BF), ("r32", 64, BF), ("tri", 64, BF), ("cq", 80, BF), ("alt", 2 * C, BF),
+        ("wi", 20, F32), ("wu", 80, F32), ("mask", 336, BF), ("keep", C, BF), ("cut", 336, BF), ("cols", C, F32),
+        ("half", C, BF), ("tp", C, F32), ("qa", 80, BF), ("qq", 80, BF), ("qs", 80, F32), ("sg", 20 * C, BF),
+        ("ft", 5 * 1280, BF), ("m1", C, F16), ("m2", C, F16), ("sti", 512, BF),
+        ("un", 1280, BF), ("sn", 1280, BF), ("m3", C, BF), ("m4", C, BF), ("td", 80, F32),
+        ("os_", 20, U16), ("of_", 20, U16), ("vw", 656, F32), ("y1", 336, F32),
         ("ki", 20, I32), ("kj", 20, I32), ("do_", 1280, BF), ("dp", 1280, BF), ("df", 1280, BF),
         ("zo", 1280, BF), ("zi", 1280, BF), ("z", 1280, BF), ("hs", 4 * HW, BF), ("hp", 1280, BF),
-        ("fr", C, F32), ("fm", C, F32), ("fo", C, F32), ("yo", C, F32)]:
+        ("fr", 2 * C, BF), ("fm", 2 * C, BF), ("fo", C, F32), ("yo", C, F32)]:
     _sb(_n, _w, _d)
-for _n, _w in [("u", 128), ("up", 256), ("v", 128), ("w", 512), ("e", 512), ("s", 128), ("f", 5 * C), ("z", C), ("h", C)]:
+for _n, _w in [("u", 128), ("up", 384), ("v", 128), ("w", 512), ("e", 512), ("s", 128), ("f", 5 * C), ("z", C), ("h", C)]:
     _pair("c" + _n, _w)
 for _t in range(R + 1):
     _pair("t%d" % _t, C)
@@ -158,8 +166,9 @@ def rank_program(g, core, T, topo):
         if bias is not None:
             kw["bias"] = bias[0] if isview(bias) else bias
         if scale is not None:
-            kw["scale"] = scale
-        run("A", lambda: g.scalar.activation(out[0], in_[0], func, **kw), [out], [in_] + ([bias] if isview(bias) else []))
+            kw["scale"] = scale[0] if isview(scale) else scale
+        run("A", lambda: g.scalar.activation(out[0], in_[0], func, **kw), [out],
+            [in_] + [x for x in (bias, scale) if isview(x)])
 
     def move(on_vector, out, in_):
         if on_vector:
@@ -202,63 +211,70 @@ def rank_program(g, core, T, topo):
             count["sent"] = count.get("sent", 0) + n
         note("X", sem, len(topo.engines(peer, core)) * len(jobs), [j[0] for j in jobs], [])
 
-    XP, ZP, SP = [(0, XC), (XC, C)], [(0, ZC), (ZC, C)], [(0, C // 2), (C // 2, C)]
+    XP, ZP, LP = [(0, XC), (XC, C)], [(0, ZC), (ZC, C)], [(LC, C), (0, LC)]
+    E = [pair("ce", 128 * b, 128 * b + 128) for b in range(4)]
+    W = [pair("cw", 128 * b, 128 * b + 128) for b in range(4)]
+    UP = [pair("cup", 128 * k, 128 * k + 128) for k in range(3)]
+    p16, p32, p4, run32 = [view("pf", k, k + 1) for k in range(4)]
+
     load("A", "du", [(view("ut"), T.u[:])])
     for i, (a, b) in enumerate(XP):
         load("S", "dx%d" % i, [(view("x0", 4 * a, 4 * b), T.x[:, 4 * a:4 * b])])
-    iota(view("ioff"), [[16, 2], [32, 4], [0, 2]], 0, 0)
-    iota(view("pc", 0, 1), [[1, 1]], 0, 1)
-    iota(view("r32"), [[1, 32], [0, 2]], 0, 0)
-    iota(view("r16"), [[0, 20], [1, 16]], 0, 0)
-    iota(view("wi"), [[16, 20]], 0, 0)
     fill(view("ones"), 1.0)
-    fill(view("st"), 0.0)
-    copy(view("uoff"), view("ioff"))
+    iota(view("pc", 0, 1), [[1, 1]], 0, 1)
+    iota(view("ioff", 0, 16), [[16, 2], [32, 4], [0, 2]], 0, 0)
+    iota(view("ioff", 16, 24), [[16, 8]], 0, 0)
+    iota(view("sti"), [[1, 8], [0, 32], [-1, 2]], 0, 0)
+    run("G", lambda: g.affine_select(T.eye[:], T.ones[:, 0:128], [[1, 128]], A.is_equal, 0.0, 0, -1),
+        [view("eye")], [view("ones", 0, 128)])
+    iota(view("r32"), [[1, 32], [0, 2]], 0, 0)
+    iota(view("wi"), [[16, 20]], 164, 0)
+    iota(view("r16"), [[0, 21], [1, 16]], 0, 0)
+    for b in range(4):
+        act(view("et", 512 * b, 512 * b + 512), view("ones"), F.Copy, None, 0.0)
     ts(view("pm", 0, 1), view("pc", 0, 1), 15, A.bitwise_and)
     ts(view("pm", 1, 2), view("pc", 0, 1), 31, A.bitwise_and)
-    for a in range(4):
-        for h in range(2):
-            o = 4 * (32 * a + 16 * h) + h
-            fill(view("st", o, o + 64 - h, 2, (32 * a, 32 * a + 32)), 512.0)
-    copy(view("pf", 0, 2), view("pm", 0, 2))
+    ts(view("pm", 2, 3), view("pc", 0, 1), 15, A.bitwise_and, 2, A.logical_shift_right)
+    ts(view("pm", 3, 4), view("pc", 0, 1), 5, A.logical_shift_right)
     fill(view("cq"), 8.0)
+    copy(view("pf", 0, 4), view("pm", 0, 4))
+    copy(view("uoff", 0, 16), view("ioff", 0, 16))
+    ts(view("uoff", 16, 24), view("ioff", 16, 24), p4, A.add)
+    fill(view("cq", 1, 80, 4), 1.0)
+    fill(view("wu"), 4096.0)
+    fill(view("half"), -0.5)
+    fill(view("hs", 15, 4 * HW, HW), 0.0)
+    fill(view("wu", 1, 80, 4), -4096.0)
+    ts(view("st"), view("sti"), 0.5, A.mult, run32, A.is_equal)
+    for b in range(4):
+        act(view("et", 512 * b + b, 512 * b + 512, 4), view("eye"), F.Copy)
+    ts(view("tri"), view("r32"), p32, A.is_gt, 0.5, A.subtract)
     quant(pair("cs"), view("st"))
-    ts(view("tri"), view("r32"), view("pf", 1, 2), A.is_gt, 0.5, A.subtract)
-    fill(view("cq", 1, C, 16), 1.0)
-    fill(view("half"), 0.5)
-    fill(view("wu"), 0.0)
-    fill(view("alt"), 1.0)
-    fill(view("hs", C, 4 * HW, HW), 0.0)
-    ts(view("mk16"), view("r16"), view("pf", 0, 1), A.is_equal, 1.0 / 512, A.mult)
-    ts(view("kp16"), view("r16"), 1.0, A.min)
-    for name, n in (("un", 1280), ("vw", C)):
-        for a in range(0, n, 512):
-            act(view(name, a, min(n, a + 512)), view("ones", 0, min(n, a + 512) - a), F.Copy, None, 0.0)
-
-    def later():
-        ts(view("mask"), view("r16"), view("pf", 0, 1), A.is_equal)
-        ts(view("cbig"), view("r16"), view("pf", 0, 1), A.is_equal, 2.0 ** 21, A.mult)
-        ts(view("keep"), view("r16"), 1.0, A.min)
-        ts(view("wu", 1, 40, 2), view("wi"), view("pf", 0, 1), A.add)
-        fill(view("alt", 0, 2 * C, 2), 0.0)
-
-    def unit(b):
-        out, src = view("et", 512 * b, 512 * b + 512), view("ones")
-        run("G", lambda: g.affine_select(out[0], src[0], [[1, 512]], A.is_equal, 0.0, -b, -4), [out], [src])
-
-    unit(0)
-    unit(1)
+    ts(view("wu", 3, 80, 4), view("wi"), p16, A.add)
     quant(pair("cu"), view("ut"))
-    copy(cast(view("cupq"), dt.uint32), by(cast(view("cuq"), dt.uint32), view("uoff")))
-    act(view("cups"), by(view("cus"), view("uoff")), F.Copy)
-    for a, b in XP:
-        quant(pair("t0", a, b), view("x0", 4 * a, 4 * b))
-    order("S", [], [view("x0")])
-    load("S", "dw", [(cast(view("cwq"), dt.uint8), T.wc[:]), (view("cws"), T.ws[:])])
-    load("S", "dv", [(view("vt"), T.v[:])])
+    for a, b in ((16, 24), (0, 16)):
+        copy(cast(view("cupq", 16 * a, 16 * b), dt.uint32), by(cast(view("cuq"), dt.uint32), view("uoff", a, b)))
+        act(view("cups", 16 * a, 16 * b), by(view("cus"), view("uoff", a, b)), F.Copy)
+    act(view("keep"), view("r16", 0, C), F.Sign)
 
-    E = [pair("ce", 128 * b, 128 * b + 128) for b in range(4)]
-    W = [pair("cw", 128 * b, 128 * b + 128) for b in range(4)]
+    def prices(name, i):
+        a, b = XP[i]
+        mm(bank(SCO[i], b - a), UP[2], pair(name, a, b))
+
+    def turn(i):
+        a, b = XP[i]
+        src, dst = bank(SCO[i], b - a), view("tp", a, b)
+        run("V", lambda: g.vector.transpose(dst[0], src[0]), [dst], [src])
+
+    def lots(i):
+        a, b = XP[i][0] // 4, XP[i][1] // 4
+        return [lambda: ts(view("qa", a, b), view("tp", 4 * a, 4 * b, 4), 0.0, A.is_gt),
+                lambda: scan(view("qq", a, b), view("cq", a, b), view("qa", a, b), 1.0, A.min, A.add)]
+
+    quant(pair("t0", 0, XC), view("x0", 0, 4 * XC))
+    prices("t0", 0)
+    quant(pair("ce", 0, 256), view("et", 0, 1024))
+    quant(pair("t0", XC, C), view("x0", 4 * XC, 4 * C))
 
     for t in range(R):
         mate = rank ^ STEP[t]
@@ -266,107 +282,162 @@ def rank_program(g, core, T, topo):
         buys = rank < mate
         mine, theirs = "t%d" % t, "l%d" % t
         lo, la, li, lb = [view("%s%d" % (n, t)) for n in ("lo", "la", "li", "lb")]
-        first = C if topo.chip(core) == topo.chip(peer) else XC
+        first = C if topo.chip(core) == topo.chip(peer) else TC
 
         def hand(a, b):
             send(peer, "aT%d" % t, [(cast(view(theirs + "q", a, b), dt.uint8), cast(view(mine + "q", a, b), dt.uint8)),
                                     (view(theirs + "s", a, b), view(mine + "s", a, b))])
 
-        mm(bank(0, XC), pair("cu"), pair(mine, 0, XC))
-        mm(bank(3, C - XC), pair("cu"), pair(mine, XC, C))
-        mm(bank(1), pair("cup", 0, 128), pair(mine))
-        mm(bank(2), pair("cup", 128, 256), pair(mine))
+        turn(0)
+        for step in lots(0):
+            step()
+        mm(bank(ROW[0]), UP[0], pair(mine))
+        prices(mine, 1)
+        mm(bank(ROW[1]), UP[1], pair(mine))
         hand(0, first)
-        for i, (a, b) in enumerate(XP):
-            src, dst = bank(3 * i, b - a), view("tp", a, b)
-            run("V", lambda: g.vector.transpose(dst[0], src[0]), [dst], [src])
-            ts(view("qa", a, b), dst, 0.0, A.is_gt)
-            scan(view("qq", a, b), view("cq", a, b), view("qa", a, b), 1.0, A.min, A.add)
         if t == 0:
-            unit(2)
-            unit(3)
-            iota(view("keyj"), [[1, C]], 512, 0)
-        else:
-            for b in range(4):
-                mm(bank(OWN[b]), E[b], pair(mine))
-        cmp_, tie, loose = (A.is_gt, A.add, -0.5) if buys else (A.is_lt, A.subtract, 0.5)
+            iota(view("un"), [[0, 1280]], 0, 0)
+            quant(pair("ce", 256, 512), view("et", 1024, 2048))
+            ts(view("mask"), view("r16"), p16, A.is_equal)
+        for b in range(4):
+            mm(bank(OWN[b]), E[b], pair(mine))
+        cmp_, loose = (A.is_gt, -0.5) if buys else (A.is_lt, 0.5)
 
-        def total(w):
-            final = w == TURN[-1] // 2
-            for a, b in (SP if final else [(0, C)]):
-                quant(pair("cf", C * w + a, C * w + b), view("ft", 1280 * w + 4 * a, 1280 * w + 4 * b))
-            for i, (a, b) in enumerate(SP):
-                mm(bank(SUM[i], b - a), pair("cs"), pair("cf", C * w + a, C * w + b), w == TURN[0] // 2, final)
+        def signs(b, h, a0, a1):
+            s0 = 2 * C * b + h
+            return view("sg", s0 + 2 * a0, s0 + 2 * a1 - 1, 2)
 
-        def earlier(m, a0, a1, lim):
-            s0, f0 = 2 * C * (m // 2) + m % 2, 1280 * (m // 4) + m % 4
+        def flags(b, h, a0, a1):
+            f0 = 1280 * (b // 2) + 2 * (b % 2) + h
+            return view("ft", f0 + 4 * a0, f0 + 4 * a1 - 3, 4)
+
+        def sign(b, h, a0, a1):
+            m = 2 * b + h
+            act(signs(b, h, a0, a1), bank(ROW[h], a1, a0), F.Sign, view("tp", 16 * m, 16 * m + 1), -1.0)
+
+        def earlier(b, h, a0, a1, lim):
+            m = 2 * b + h
             if a1 > a0:
-                ts(view("ft", f0 + 4 * a0, f0 + 4 * a1 - 3, 4), view("sg", s0 + 2 * a0, s0 + 2 * a1 - 1, 2), lim, cmp_,
-                   view("qq", 16 * m + 3, 16 * m + 4), A.mult)
+                ts(flags(b, h, a0, a1), signs(b, h, a0, a1), lim, cmp_, view("qq", 4 * m + 3, 4 * m + 4), A.mult)
 
-        for n, b in enumerate(TURN):
-            cut = 0 if b == 0 else (32 * b + 32 if b < 5 or b == 9 else 32 * b)
-            parts = [(cut, C, loose), (0, cut, 0.0)]
-            if cut == 32 * b:
-                parts.reverse()
-            s0 = 2 * C * b
+        def parts(b):
+            a0 = LC if b in LATE else 0
+            lo_, hi_ = 32 * b, 32 * b + 32
+            if lo_ == a0 or (hi_ != C and lo_ - a0 >= C - hi_):
+                return (a0, lo_, 0.0), (lo_, C, loose)
+            return (hi_, C, loose), (a0, hi_, 0.0)
+
+        def free(b, h):
+            earlier(b, h, *parts(b)[0])
+
+        def direct(b, h):
+            m, (a0, a1, lim) = 2 * b + h, parts(b)[0]
+            op = [[A.is_gt, A.is_ge], [A.is_lt, A.is_le]][buys][lim != 0.0]
+            copy(view("qs", 4 * m + 3, 4 * m + 4), view("qq", 4 * m + 3, 4 * m + 4))
+            ts(flags(b, h, a0, a1), bank(ROW[h], a1, a0), view("tp", 16 * m, 16 * m + 1), op,
+               view("qs", 4 * m + 3, 4 * m + 4), A.mult)
+
+        def strict(b, h):
+            m = 2 * b + h
+            act(flags(b, h, 0, LC), signs(b, h, 0, LC), F.Relu, None, view("qs", 4 * m + 3, 4 * m + 4))
+
+        def ties(b):
+            d = view("sg", 2 * C * b + 64 * b, 2 * C * b + 64 * b + 64)
+            tt(d, d, view("tri"), A.add if buys else A.subtract)
+
+        def tied(b):
             for h in range(2):
-                m = 2 * b + h
-                act(view("sg", s0 + h, s0 + 2 * C, 2), bank(1 + h), F.Sign, view("tp", 16 * m, 16 * m + 1), -1.0)
-                if h:
-                    d = view("sg", s0 + 64 * b, s0 + 64 * b + 64)
-                    tt(d, d, view("tri"), tie)
-                earlier(m, *parts[0])
-            if n % 2 == 0 and n:
-                total(TURN[n - 1] // 2)
+                earlier(b, h, *parts(b)[1])
+
+        def total(w, pieces):
+            a0, a1 = LP[pieces[-1]][0], LP[pieces[0]][1]
+            quant(pair("cf", C * w + a0, C * w + a1), view("ft", 1280 * w + 4 * a0, 1280 * w + 4 * a1))
+            for i in pieces:
+                a, b = LP[i]
+                mm(bank(SUM[i], b - a), pair("cs"), pair("cf", C * w + a, C * w + b), w == TURN[0] // 2, w == TURN[-1] // 2)
+
+        for b in TURN[:HEAD]:
+            sign(b, 0, 0, C)
+        turn(1)
+        lots(1)[0]()
+        direct(TURN[0], 1)
+        lots(1)[1]()
+        sign(TURN[0], 1, *parts(TURN[0])[1][:2])
+        for b in TURN[1:HEAD]:
+            sign(b, 1, 0, C)
+        for b in TURN[:HEAD]:
+            free(b, 0)
+        ties(TURN[0])
+        for n, b in enumerate(TURN[1:], 1):
+            if b == LATE[-1]:
+                act(view("qs", 48, 80), view("qq", 48, 80), F.Copy, None, 1.0 if buys else -1.0)
+            if n >= HEAD:
+                for h in range(2):
+                    sign(b, h, 0, C)
+                free(b, 0)
+            tied(TURN[n - 1])
+            free(b, 1)
+            ties(b)
+            if n % 2 == 0:
+                total(TURN[n - 1] // 2, [0] if TURN[n - 1] in LATE else [0, 1])
+        for b in LATE:
             for h in range(2):
-                earlier(2 * b + h, *parts[1])
-        total(TURN[-1] // 2)
-        for i, (a, b) in enumerate(SP):
-            tt(view("m1", a, b), bank(SUM[i], b - a), view("mk16", a, b), A.mult)
-        scan(view("m2"), view("kp16"), view("m1"), 0.0, A.mult, A.add)
+                strict(b, h)
+        tied(LATE[-1])
+        total(LATE[0] // 2, [1])
+        total(LATE[-1] // 2, [0])
+        total(LATE[-1] // 2, [1])
+        for i, (a, b) in enumerate(LP):
+            tt(view("m1", a, b), bank(SUM[i], b - a), view("mask", a, b), A.mult)
+        scan(view("m2"), view("keep"), view("m1"), 0.0, A.mult, A.add)
         copy(lo, view("m2", 15, C, 16))
         send(peer, "aA%d" % t, [(la, lo)])
         if first < C:
             hand(first, C)
 
         if t == 0:
-            quant(pair("ce"), view("et"))
-            for b in range(4):
-                mm(bank(OWN[b]), E[b], pair(mine))
-        for i, (a, b) in enumerate(SP):
-            tt(view("key", a, b), bank(SUM[i], b - a), view("keyj", a, b), A.add)
+            iota(view("cols"), [[1, C]], 0, 0)
+            iota(view("vw", 0, 336), [[0, 336]], -16384, 0)
+            iota(view("alt"), [[0, C], [1, 2]], 0, 0)
+            act(view("cut"), view("mask"), F.Identity, 512.0, -2.0 ** 20)
         scatter(view("un"), lo, view("half"))
-        if t == 0:
-            later()
         for b in range(4):
             mm(bank(FAR[b]), E[b], pair(theirs))
         for b in range(4):
             act(view("do_", C * b, C * b + C), bank(OWN[b]), F.Copy, None, 0.5)
-            act(view("df", C * b + XC, C * b + C), bank(OWN[b], C, XC), F.Copy)
+            for i, (a0, a1) in enumerate(XP):
+                if b not in ACC[i]:
+                    act(view("df", C * b + a0, C * b + a1), bank(OWN[b], a1, a0), F.Copy)
         for b in range(4):
             act(view("dp", C * b, C * b + C), bank(FAR[b]), F.Copy, None, 0.5)
 
+        if t == 0:
+            order("S", [], [la])
+            load("S", "dw", [(cast(view("cwq"), dt.uint8), T.wc[:]), (view("cws"), T.ws[:])])
+        if t == 1:
+            order("S", [], [la])
+            load("S", "dv", [(view("vt"), T.v[:])])
         scatter(view("un"), la, view("half"))
-        scan(view("sn"), view("un"), view("un"), -161.0, A.add, A.add)
-        tt(view("m3"), by(view("sn"), lo), view("mask"), A.mult)
+        scan(view("sn"), view("un"), view("un"), 160.0, A.add, A.add)
+        tt(view("m3"), by(view("sn"), lo), view("mask", 0, C), A.mult)
+        if t + 1 == R:
+            act(view("fr", 0, 2 * C, 2), by(view("sn"), lo), F.Copy)
+            act(view("fr", 1, 2 * C, 2), view("fr", 0, 2 * C, 2), F.Relu, -160.5 * 4096, -4096.0)
         scan(view("m4"), view("keep"), view("m3"), 0.0, A.mult, A.add)
         seg = view("m4", 15, C, 16)
-        ts(view("ta", 0, 40, 2), seg, 160.0, A.is_ge, 1024.0, A.mult)
-        ts(view("ta", 1, 40, 2), seg, 160.0, A.add, float(C), A.min)
-        scan(view("td"), view("wu"), view("ta"), 0.0, A.min, A.add)
-        copy(view("os_"), view("td", 1, 40, 2))
-        scatter(view("vw"), view("os_"), view("key"))
-        scan(view("y1"), view("vw", 0, C), view("vw", 0, C), 0.0, A.max, A.max)
-        scan(view("y2"), view("cbig"), view("y1"), 0.0, A.max, A.min)
-        copy(view("ki"), view("y2", 15, C, 16))
+        ts(view("m4", 11, C, 16), seg, 160.5, A.add, -4096.0, A.mult)
+        scan(view("td"), view("m4", 3, C, 4), view("wu"), 0.0, A.max, A.min)
+        ts(view("os_"), view("td", 3, 80, 4), 160.0, A.add)
+        scatter(view("vw"), view("os_"), view("cols"))
+        scan(view("y1", 0, 324), view("cut", 0, 324), view("vw", 0, 324), 0.0, A.add, A.max)
+        tt(view("ki"), view("y1", 15, C, 16), view("y1", 18, C + 3, 16), A.max)
         ts(view("kj"), view("ki"), 511, A.bitwise_and)
         copy(li, view("kj"))
         send(peer, "aB%d" % t, [(lb, li)])
 
         if t + 1 < R:
             iota(view("un"), [[0, 1280]], 0, 0)
-            iota(view("vw", 0, C), [[0, C]], 0, 0)
+            iota(view("vw", 0, 336), [[0, 336]], -16384, 0)
         for b in range(4):
             for a0, a1 in ([(0, C)] if b < 2 else ZP):
                 if b in SPLIT[a0 > 0]:
@@ -374,16 +445,11 @@ def rank_program(g, core, T, topo):
                 else:
                     out = view("zo", C * b + a0, C * b + a1)
                 move(b >= 2, out, by(view("do_", C * b, C * b + C), view("li%d" % t, a0 // 16, a1 // 16)))
-        copy(view("of_"), view("ta", 1, 40, 2))
-        if t == 0:
+        ts(view("of_"), seg, -161.0, A.max, 176.0, A.add)
+        if t == 1:
             quant(pair("cv"), view("vt"))
         if t + 1 == R:
-            act(view("fr"), by(view("sn"), lo), F.Identity, 161.0)
-            ts(view("fm"), view("fr"), C + 0.5, A.is_lt)
-            tt(view("fo"), view("fr"), view("fm"), A.mult)
-            ts(view("fo"), view("fo"), -1.0, A.add)
-            for k in range(8):
-                store("S", T.ol[k:k + 1, :], view("fo", 0, C, 1, (16 * k, 16 * k + 1)))
+            scan(view("fm"), view("alt"), view("fr"), 0.0, A.mult, A.subtract)
 
         def far(b, a0, a1):
             return by(view("dp", C * b, C * b + C), view("lb%d" % t, a0 // 16, a1 // 16))
@@ -392,46 +458,59 @@ def rank_program(g, core, T, topo):
             for b in SPLIT[i]:
                 o = 2 * C * (b - 2)
                 act(view("zi", o + 2 * a0 + 1, o + 2 * a1, 2), far(b, a0, a1), F.Copy)
+        for i, b in JOINT:
+            a0, a1 = ZP[i]
+            if b is None:
+                quant(pair("cz", a0, a1), view("z", 4 * a0, 4 * a1))
+            elif b in SPLIT[i]:
+                o = 2 * C * (b - 2)
+                scan(view("z", 4 * a0 + b - 2, 4 * a1, 2), view("alt", 2 * a0, 2 * a1),
+                     view("zi", o + 2 * a0, o + 2 * a1), 0.0, A.mult, A.add)
+            else:
+                tt(view("z", 4 * a0 + b, 4 * a1, 4), far(b, a0, a1), view("zo", C * b + a0, C * b + a1), A.add)
         for i, (a0, a1) in enumerate(ZP):
-            for b in ([0, 2, 3, 1] if i == 0 else [2, 3, 0, 1]):
-                if b in SPLIT[i]:
-                    o = 2 * C * (b - 2)
-                    scan(view("z", 4 * a0 + b - 2, 4 * a1, 2), view("alt", 2 * a0, 2 * a1),
-                         view("zi", o + 2 * a0, o + 2 * a1), 0.0, A.mult, A.add)
-                else:
-                    tt(view("z", 4 * a0 + b, 4 * a1, 4), far(b, a0, a1), view("zo", C * b + a0, C * b + a1), A.add)
-            quant(pair("cz", a0, a1), view("z", 4 * a0, 4 * a1))
             for b in range(4):
                 mm(bank(4 * i + b, a1 - a0), W[b], pair("cz", a0, a1))
-        for i, (a0, a1) in enumerate(ZP):
-            for b in range(4):
-                out = view("hs", HW * b + a0, HW * b + a1)
-                if i and b == 0:
+        if t + 1 == R:
+            ts(view("fo"), view("fm", 1, 2 * C, 2), 159.0, A.add, -1.0, A.max)
+            for k in range(8):
+                store("S", T.ol[k:k + 1, :], view("fo", 0, C, 1, (16 * k, 16 * k + 1)))
+
+        for q, what, i, b in AFTER:
+            if what == "r":
+                a0, a1 = ZP[i]
+                out = view("hs", HW * b + 16 + a0, HW * b + 16 + a1)
+                if q == "V":
                     ts(out, bank(4 * i + b, a1 - a0), 0.0, A.max, 0.03125, A.mult)
                 else:
                     act(out, bank(4 * i + b, a1 - a0), F.Relu, None, 0.03125)
-
-        nxt = "t%d" % (t + 1)
-        for b in range(4):
-            mm(bank(b, XC), E[b], pair(mine, 0, XC), True, False)
+            a0, a1 = XP[i]
+            if what == "g":
+                move(q == "V", view("hp", 4 * a0 + b, 4 * a1, 4),
+                     by(view("hs", HW * b, HW * b + HW), view("of_", a0 // 16, a1 // 16)))
+            if what == "q":
+                quant(pair("ch", a0, a1), view("hp", 4 * a0, 4 * a1))
         for i, (a0, a1) in enumerate(XP):
-            for j, b in ([(0, 0), (0, 1), (0, 2), (0, 3), (1, 0)] if i == 0 else [(1, 1), (1, 2), (1, 3)]):
-                move(b % 2 == 0, view("hp", 4 * XP[j][0] + b, 4 * XP[j][1], 4),
-                     by(view("hs", HW * b, HW * b + HW), view("of_", XP[j][0] // 16, XP[j][1] // 16)))
-            quant(pair("ch", a0, a1), view("hp", 4 * a0, 4 * a1))
+            for b in ACC[i]:
+                mm(bank(4 * i + b, a1 - a0), E[b], pair(mine, a0, a1), True, False)
+        nxt = "t%d" % (t + 1)
+        for i, (a0, a1) in enumerate(XP):
             for b in range(4):
-                mm(bank(4 * i + b, a1 - a0), E[b], pair("ch", a0, a1), i == 1, True)
-        for b in range(4):
-            act(view("xs", b, 4 * XC, 4), bank(b, XC), F.Copy)
-        for b in range(4):
-            tt(view("xs", 4 * XC + b, 4 * C, 4), bank(4 + b, C - XC), view("df", C * b + XC, C * b + C), A.add)
-            if b == 0:
-                quant(pair(nxt, 0, XC), view("xs", 0, 4 * XC))
-        quant(pair(nxt, XC, C), view("xs", 4 * XC, 4 * C))
+                mm(bank(4 * i + b, a1 - a0), E[b], pair("ch", a0, a1), b not in ACC[i], True)
+                out = view("xs", 4 * a0 + b, 4 * a1, 4)
+                if b in ACC[i]:
+                    act(out, bank(4 * i + b, a1 - a0), F.Copy)
+                else:
+                    tt(out, bank(4 * i + b, a1 - a0), view("df", C * b + a0, C * b + a1), A.add)
+            if i and t + 1 < R:
+                prices(nxt, 0)
+            elif i:
+                mm(bank(0, XC), pair("cv"), pair(nxt, 0, XC))
+            quant(pair(nxt, a0, a1), view("xs", 4 * a0, 4 * a1))
 
     last = "t%d" % R
+    mm(bank(1, C - XC), pair("cv"), pair(last, XC, C))
     for i, (a0, a1) in enumerate(XP):
-        mm(bank(i, a1 - a0), pair("cv"), pair(last, a0, a1))
         store("S", T.oc[:, 4 * a0:4 * a1], cast(view(last + "q", a0, a1), dt.uint8))
     act(view("yo", 0, XC), bank(0, XC), F.Copy)
     store("A", T.y[:, 0:XC], view("yo", 0, XC))

@@ -3,19 +3,19 @@ from concourse.mybir import dt, AluOpType, ActivationFunctionType
 
 C, R, STEP = 320, 3, [1, 2, 4]
 ZC, XC = 160, 160
-TC = 192
+TC = 160
 HW = 336
 Q4, U8, BF, F32, I32, U16, F16 = "float8_e4m3fn_x4", "uint8", "bfloat16", "float32", "int32", "uint16", "float16"
 ROW, SCO, SUM = [1, 2], [0, 3], [7, 3]
 OWN, FAR = [4, 5, 6, 0], [1, 2, 7, 3]
 SPLIT = [[3], [2, 3]]
-TURN = [2, 3, 1, 0, 4, 5, 6, 7, 8, 9]
-HEAD = 3
-LC, LATE = 128, [6, 7, 8, 9]
+TURN = [2, 3, 1, 0, 4, 5, 6, 7, 9, 8]
+HEAD, ALONE = 5, 3
+LC, LATE = 128, [6, 7, 9, 8]
 JOINT = [(0, 0), (0, 2), (0, 3), (1, 2), (0, 1), (1, 3), (0, None), (1, 0), (1, 1), (1, None)]
-AFTER = [("A", "r", 0, 0), ("A", "r", 0, 1), ("A", "r", 0, 2), ("A", "r", 0, 3), ("V", "r", 1, 0), ("A", "r", 1, 1),
-         ("V", "g", 0, 0), ("A", "r", 1, 2), ("V", "g", 0, 1), ("A", "r", 1, 3), ("A", "g", 0, 2), ("V", "g", 0, 3),
-         ("A", "g", 1, 0), ("V", "q", 0, 0), ("A", "g", 1, 1), ("V", "g", 1, 2), ("V", "g", 1, 3), ("V", "q", 1, 0)]
+AFTER = [("A", "r", 0, 0), ("A", "r", 0, 1), ("A", "r", 0, 2), ("A", "r", 0, 3), ("A", "r", 1, 0), ("V", "g", 0, 0),
+         ("A", "r", 1, 1), ("V", "g", 0, 1), ("A", "r", 1, 2), ("V", "g", 0, 2), ("A", "r", 1, 3), ("A", "g", 0, 3),
+         ("V", "g", 1, 0), ("V", "q", 0, 0), ("A", "g", 1, 1), ("V", "g", 1, 2), ("A", "g", 1, 3), ("V", "q", 1, 0)]
 ACC = [[0, 1], [0, 2]]
 
 SCRATCH = {}
@@ -33,11 +33,13 @@ def _pair(name, n):
 for _n, _w, _d in [
         ("x0", 1280, BF), ("xs", 1280, BF), ("ut", 512, BF), ("vt", 512, BF), ("et", 2048, BF), ("st", 512, BF),
         ("ones", 512, BF), ("eye", 128, BF), ("ioff", 24, F32), ("uoff", 24, U16), ("pc", 8, I32), ("pm", 8, I32),
-        ("pf", 8, F32), ("r16", 336, BF), ("r32", 64, BF), ("tri", 64, BF), ("cq", 80, BF), ("alt", 2 * C, BF),
+        ("pf", 8, F32), ("r16", 336, BF), ("r32", 64, BF), ("cq", 80, BF), ("alt", 2 * C, BF),
         ("wi", 20, F32), ("wu", 80, F32), ("mask", 336, BF), ("keep", C, BF), ("cut", 336, BF), ("cols", C, F32),
-        ("half", C, BF), ("tp", C, F32), ("qa", 80, BF), ("qq", 80, BF), ("qs", 80, F32), ("sg", 20 * C, BF),
+        ("half", C, BF), ("tp", C, F32), ("qa", 80, BF), ("qq", 80, BF), ("qs", 80, F32), ("sg", 40 * C, BF),
+        ("pos", 128, BF), ("neg", 128, BF),
         ("ft", 5 * 1280, BF), ("m1", C, F16), ("m2", C, F16), ("sti", 512, BF),
         ("un", 1280, BF), ("sn", 1280, BF), ("m3", C, BF), ("m4", C, BF), ("td", 80, F32),
+        ("s2", 656, BF), ("one", C, BF), ("ih", 20, I32), ("lh", 20, U16), ("ew", 20, F32), ("ev", 20, BF),
         ("os_", 20, U16), ("of_", 20, U16), ("vw", 656, F32), ("y1", 336, F32),
         ("ki", 20, I32), ("kj", 20, I32), ("do_", 1280, BF), ("dp", 1280, BF), ("df", 1280, BF),
         ("zo", 1280, BF), ("zi", 1280, BF), ("z", 1280, BF), ("hs", 4 * HW, BF), ("hp", 1280, BF),
@@ -53,14 +55,32 @@ for _t in range(R):
         _sb("%s%d" % (_n, _t), 20, U16)
 SCRATCH["ps"] = ("psum", [128, 4096], F32)
 
-SEMAPHORES = (["cV", "cA", "cT", "cG", "sent", "dx0", "dx1", "du", "dv", "dw", "out"]
+SEMAPHORES = (["cV", "cA", "cT", "cG", "sent", "dx0", "dx1", "du", "dv", "dw", "out", "aQ", "aS"]
               + ["%s%d" % (n, t) for t in range(R) for n in ("aT", "aA", "aB")])
+
+
+def helper(core, T, topo):
+    here = [c for c in T.cores if topo.chip(c) == topo.chip(core)]
+    spare = [c for c in topo.cores_of(core) if c not in T.cores and topo.die(c) != topo.die(core)]
+    return spare[here.index(core)]
+
+
+def hand_on(g, core, T, topo):
+    for rank, src in enumerate(T.cores):
+        for t in range(R):
+            dst = T.cores[rank ^ STEP[t]]
+            if topo.chip(src) != topo.chip(dst) and helper(src, T, topo) == core:
+                rid, pid, _ = topo.addr(dst)
+                for sem, ap in (("aQ", T["l%dq" % t][:, TC:C].bitcast(dt.uint8)), ("aS", T["l%ds" % t][:, TC:C])):
+                    g.wait_ge(T.sem[sem], len(topo.engines(src, core)))
+                    g.remote_dma(ap, ap, T.sem["aT%d" % t], T.sem.sent, pid, rid, topo.mask(core, dst))
+                g.wait_ge(T.sem.sent, 2 * len(topo.engines(core, dst)))
 
 
 def rank_program(g, core, T, topo):
     rank = T.rank_of(core)
     if rank is None:
-        return
+        return hand_on(g, core, T, topo)
     A = AluOpType
     F = ActivationFunctionType
     queue = {"V": g.vector, "A": g.scalar, "T": g.tensor, "G": g, "S": g.sync}
@@ -202,14 +222,14 @@ def rank_program(g, core, T, topo):
         queue[q].dma_start(dst, src[0]).then_inc(T.sem.out, 16)
         count["out"] = count.get("out", 0) + 16
 
-    def send(peer, sem, jobs):
-        rid, pid, _ = topo.addr(peer)
-        n = len(topo.engines(core, peer))
-        for dst, src in jobs:
+    def send(peer, sem, jobs, helped=False):
+        to, last = (helper(core, T, topo), helper(peer, T, topo)) if helped else (peer, peer)
+        rid, pid, _ = topo.addr(to)
+        for (dst, src), there in zip(jobs, ("aQ", "aS") if helped else (sem, sem)):
             order("G", [], [src])
-            g.remote_dma(dst[0], src[0], T.sem[sem], T.sem.sent, pid, rid, topo.mask(core, peer))
-            count["sent"] = count.get("sent", 0) + n
-        note("X", sem, len(topo.engines(peer, core)) * len(jobs), [j[0] for j in jobs], [])
+            g.remote_dma(dst[0], src[0], T.sem[there], T.sem.sent, pid, rid, topo.mask(core, to))
+            count["sent"] = count.get("sent", 0) + len(topo.engines(core, to))
+        note("X", sem, len(topo.engines(last, core)) * len(jobs), [j[0] for j in jobs], [])
 
     XP, ZP, LP = [(0, XC), (XC, C)], [(0, ZC), (ZC, C)], [(LC, C), (0, LC)]
     E = [pair("ce", 128 * b, 128 * b + 128) for b in range(4)]
@@ -224,11 +244,12 @@ def rank_program(g, core, T, topo):
     iota(view("pc", 0, 1), [[1, 1]], 0, 1)
     iota(view("ioff", 0, 16), [[16, 2], [32, 4], [0, 2]], 0, 0)
     iota(view("ioff", 16, 24), [[16, 8]], 0, 0)
+    iota(view("r32"), [[1, 32], [0, 2]], 0, 0)
     iota(view("sti"), [[1, 8], [0, 32], [-1, 2]], 0, 0)
     run("G", lambda: g.affine_select(T.eye[:], T.ones[:, 0:128], [[1, 128]], A.is_equal, 0.0, 0, -1),
         [view("eye")], [view("ones", 0, 128)])
-    iota(view("r32"), [[1, 32], [0, 2]], 0, 0)
-    iota(view("wi"), [[16, 20]], 164, 0)
+    iota(view("pos"), [[0, 64], [1, 2]], 0, 0)
+    iota(view("neg"), [[0, 64], [-1, 2]], 0, 0)
     iota(view("r16"), [[0, 21], [1, 16]], 0, 0)
     for b in range(4):
         act(view("et", 512 * b, 512 * b + 512), view("ones"), F.Copy, None, 0.0)
@@ -241,21 +262,18 @@ def rank_program(g, core, T, topo):
     copy(view("uoff", 0, 16), view("ioff", 0, 16))
     ts(view("uoff", 16, 24), view("ioff", 16, 24), p4, A.add)
     fill(view("cq", 1, 80, 4), 1.0)
-    fill(view("wu"), 4096.0)
-    fill(view("half"), -0.5)
-    fill(view("hs", 15, 4 * HW, HW), 0.0)
-    fill(view("wu", 1, 80, 4), -4096.0)
+    fill(view("keep"), 1.0)
+    for b in TURN:
+        ts(view("sg", 4 * C * b + 128 * b, 4 * C * b + 128 * b + 128, 2), view("r32"), p32, A.is_gt, 0.5, A.subtract)
     ts(view("st"), view("sti"), 0.5, A.mult, run32, A.is_equal)
+    fill(view("keep", 0, C, 16), 0.0)
+    quant(pair("cs"), view("st"))
     for b in range(4):
         act(view("et", 512 * b + b, 512 * b + 512, 4), view("eye"), F.Copy)
-    ts(view("tri"), view("r32"), p32, A.is_gt, 0.5, A.subtract)
-    quant(pair("cs"), view("st"))
-    ts(view("wu", 3, 80, 4), view("wi"), p16, A.add)
     quant(pair("cu"), view("ut"))
     for a, b in ((16, 24), (0, 16)):
         copy(cast(view("cupq", 16 * a, 16 * b), dt.uint32), by(cast(view("cuq"), dt.uint32), view("uoff", a, b)))
         act(view("cups", 16 * a, 16 * b), by(view("cus"), view("uoff", a, b)), F.Copy)
-    act(view("keep"), view("r16", 0, C), F.Sign)
 
     def prices(name, i):
         a, b = XP[i]
@@ -282,30 +300,36 @@ def rank_program(g, core, T, topo):
         buys = rank < mate
         mine, theirs = "t%d" % t, "l%d" % t
         lo, la, li, lb = [view("%s%d" % (n, t)) for n in ("lo", "la", "li", "lb")]
-        first = C if topo.chip(core) == topo.chip(peer) else TC
 
-        def hand(a, b):
+        def hand(a, b, helped=False):
             send(peer, "aT%d" % t, [(cast(view(theirs + "q", a, b), dt.uint8), cast(view(mine + "q", a, b), dt.uint8)),
-                                    (view(theirs + "s", a, b), view(mine + "s", a, b))])
+                                    (view(theirs + "s", a, b), view(mine + "s", a, b))], helped)
 
         turn(0)
-        for step in lots(0):
-            step()
+        if t == 0:
+            quant(pair("ce", 256, 512), view("et", 1024, 2048))
+        lots(0)[0]()
         mm(bank(ROW[0]), UP[0], pair(mine))
         prices(mine, 1)
         mm(bank(ROW[1]), UP[1], pair(mine))
-        hand(0, first)
+        if topo.chip(core) == topo.chip(peer):
+            hand(0, C)
+        else:
+            hand(0, TC)
+            hand(TC, C, True)
         if t == 0:
             iota(view("un"), [[0, 1280]], 0, 0)
-            quant(pair("ce", 256, 512), view("et", 1024, 2048))
-            ts(view("mask"), view("r16"), p16, A.is_equal)
+            iota(view("one"), [[0, C]], -1, 0)
+            iota(view("s2", 0, 1), [[0, 1]], 160, 0)
+            iota(view("wu"), [[0, 20], [8192, 2], [0, 2]], -4096, 0)
+            iota(view("wi"), [[16, 20]], 164, 0)
         for b in range(4):
             mm(bank(OWN[b]), E[b], pair(mine))
         cmp_, loose = (A.is_gt, -0.5) if buys else (A.is_lt, 0.5)
 
         def signs(b, h, a0, a1):
-            s0 = 2 * C * b + h
-            return view("sg", s0 + 2 * a0, s0 + 2 * a1 - 1, 2)
+            s0 = 4 * C * b + 2 * h + 1
+            return view("sg", s0 + 4 * a0, s0 + 4 * a1 - 3, 4)
 
         def flags(b, h, a0, a1):
             f0 = 1280 * (b // 2) + 2 * (b % 2) + h
@@ -333,7 +357,6 @@ def rank_program(g, core, T, topo):
         def direct(b, h):
             m, (a0, a1, lim) = 2 * b + h, parts(b)[0]
             op = [[A.is_gt, A.is_ge], [A.is_lt, A.is_le]][buys][lim != 0.0]
-            copy(view("qs", 4 * m + 3, 4 * m + 4), view("qq", 4 * m + 3, 4 * m + 4))
             ts(flags(b, h, a0, a1), bank(ROW[h], a1, a0), view("tp", 16 * m, 16 * m + 1), op,
                view("qs", 4 * m + 3, 4 * m + 4), A.mult)
 
@@ -342,8 +365,8 @@ def rank_program(g, core, T, topo):
             act(flags(b, h, 0, LC), signs(b, h, 0, LC), F.Relu, None, view("qs", 4 * m + 3, 4 * m + 4))
 
         def ties(b):
-            d = view("sg", 2 * C * b + 64 * b, 2 * C * b + 64 * b + 64)
-            tt(d, d, view("tri"), A.add if buys else A.subtract)
+            d = view("sg", 4 * C * b + 128 * b, 4 * C * b + 128 * b + 128)
+            scan(d, view("pos" if buys else "neg"), d, 0.0, A.mult, A.add)
 
         def tied(b):
             for h in range(2):
@@ -358,49 +381,60 @@ def rank_program(g, core, T, topo):
 
         for b in TURN[:HEAD]:
             sign(b, 0, 0, C)
+        lots(0)[1]()
         turn(1)
+        copy(view("qs", 0, XC // 4), view("qq", 0, XC // 4))
         lots(1)[0]()
-        direct(TURN[0], 1)
+        for b in TURN[:ALONE]:
+            direct(b, 1)
         lots(1)[1]()
-        sign(TURN[0], 1, *parts(TURN[0])[1][:2])
-        for b in TURN[1:HEAD]:
-            sign(b, 1, 0, C)
+        free(TURN[0], 0)
         for b in TURN[:HEAD]:
+            sign(b, 1, *(parts(b)[1][:2] if b in TURN[:ALONE] else (0, C)))
+        for b in TURN[1:HEAD]:
             free(b, 0)
         ties(TURN[0])
         for n, b in enumerate(TURN[1:], 1):
-            if b == LATE[-1]:
-                act(view("qs", 48, 80), view("qq", 48, 80), F.Copy, None, 1.0 if buys else -1.0)
+            if n == HEAD:
+                ts(view("qs", 48, 80), view("qq", 48, 80), 1.0 if buys else -1.0, A.mult)
             if n >= HEAD:
                 for h in range(2):
                     sign(b, h, 0, C)
                 free(b, 0)
-            tied(TURN[n - 1])
-            free(b, 1)
+            if n >= ALONE:
+                free(b, 1)
             ties(b)
-            if n % 2 == 0:
-                total(TURN[n - 1] // 2, [0] if TURN[n - 1] in LATE else [0, 1])
+            if n % 2 and n > 1:
+                total(TURN[n - 2] // 2, [0] if TURN[n - 2] in LATE else [0, 1])
+            tied(TURN[n - 1])
         for b in LATE:
             for h in range(2):
                 strict(b, h)
+        if t == 0:
+            ts(view("mask"), view("r16"), p16, A.is_equal)
         tied(LATE[-1])
         total(LATE[0] // 2, [1])
         total(LATE[-1] // 2, [0])
         total(LATE[-1] // 2, [1])
         for i, (a, b) in enumerate(LP):
             tt(view("m1", a, b), bank(SUM[i], b - a), view("mask", a, b), A.mult)
-        scan(view("m2"), view("keep"), view("m1"), 0.0, A.mult, A.add)
+        for a, b in LP:
+            scan(view("m2", a, b), view("keep", a, b), view("m1", a, b), 0.0, A.mult, A.add)
         copy(lo, view("m2", 15, C, 16))
         send(peer, "aA%d" % t, [(la, lo)])
-        if first < C:
-            hand(first, C)
 
         if t == 0:
             iota(view("cols"), [[1, C]], 0, 0)
             iota(view("vw", 0, 336), [[0, 336]], -16384, 0)
             iota(view("alt"), [[0, C], [1, 2]], 0, 0)
             act(view("cut"), view("mask"), F.Identity, 512.0, -2.0 ** 20)
-        scatter(view("un"), lo, view("half"))
+            act(view("wu", 3, 80, 4), view("wi"), F.Identity, p16)
+            act(view("half"), view("one"), F.Copy, None, 0.5)
+            act(view("hs", 15, 4 * HW, HW), view("ones", 0, 4), F.Copy, None, 0.0)
+        mark = view("one" if t + 1 < R else "half")
+        if t + 1 < R:
+            ts(view("ih"), view("m2", 15, C, 16), 0.5, A.mult, 0.25, A.add)
+        scatter(view("un"), lo, mark)
         for b in range(4):
             mm(bank(FAR[b]), E[b], pair(theirs))
         for b in range(4):
@@ -417,15 +451,24 @@ def rank_program(g, core, T, topo):
         if t == 1:
             order("S", [], [la])
             load("S", "dv", [(view("vt"), T.v[:])])
-        scatter(view("un"), la, view("half"))
-        scan(view("sn"), view("un"), view("un"), 160.0, A.add, A.add)
-        tt(view("m3"), by(view("sn"), lo), view("mask", 0, C), A.mult)
-        if t + 1 == R:
+        scatter(view("un"), la, mark)
+        seg = view("m4", 15, C, 16)
+        if t + 1 < R:
+            copy(view("lh"), view("ih"))
+            scan(view("s2", 1, 641), view("un", 0, 1280, 2), view("un", 1, 1280, 2), 160.0, A.add, A.add)
+            ts(view("ew"), view("ih"), -2.0, A.mult, 1.0, A.add)
+            tt(view("m3"), by(view("s2"), view("lh")), view("mask", 0, C), A.mult)
+            tt(view("ev"), view("ew"), view("m2", 15, C, 16), A.add)
+            scan(view("m4"), view("keep"), view("m3"), 0.0, A.mult, A.add)
+            tt(seg, seg, view("ev"), A.subtract)
+        else:
+            scan(view("sn"), view("un"), view("un"), 160.0, A.add, A.add)
+            tt(view("m3"), by(view("sn"), lo), view("mask", 0, C), A.mult)
             act(view("fr", 0, 2 * C, 2), by(view("sn"), lo), F.Copy)
             act(view("fr", 1, 2 * C, 2), view("fr", 0, 2 * C, 2), F.Relu, -160.5 * 4096, -4096.0)
-        scan(view("m4"), view("keep"), view("m3"), 0.0, A.mult, A.add)
-        seg = view("m4", 15, C, 16)
+            scan(view("m4"), view("keep"), view("m3"), 0.0, A.mult, A.add)
         ts(view("m4", 11, C, 16), seg, 160.5, A.add, -4096.0, A.mult)
+        ts(view("of_"), seg, -161.0, A.max, 176.0, A.add)
         scan(view("td"), view("m4", 3, C, 4), view("wu"), 0.0, A.max, A.min)
         ts(view("os_"), view("td", 3, 80, 4), 160.0, A.add)
         scatter(view("vw"), view("os_"), view("cols"))
@@ -445,9 +488,6 @@ def rank_program(g, core, T, topo):
                 else:
                     out = view("zo", C * b + a0, C * b + a1)
                 move(b >= 2, out, by(view("do_", C * b, C * b + C), view("li%d" % t, a0 // 16, a1 // 16)))
-        ts(view("of_"), seg, -161.0, A.max, 176.0, A.add)
-        if t == 1:
-            quant(pair("cv"), view("vt"))
         if t + 1 == R:
             scan(view("fm"), view("alt"), view("fr"), 0.0, A.mult, A.subtract)
 
@@ -471,6 +511,8 @@ def rank_program(g, core, T, topo):
         for i, (a0, a1) in enumerate(ZP):
             for b in range(4):
                 mm(bank(4 * i + b, a1 - a0), W[b], pair("cz", a0, a1))
+        if t == 1:
+            quant(pair("cv"), view("vt"))
         if t + 1 == R:
             ts(view("fo"), view("fm", 1, 2 * C, 2), 159.0, A.add, -1.0, A.max)
             for k in range(8):

import numpy as np
from concourse.mybir import dt, AluOpType, ActivationFunctionType

C, R, STEP = 320, 3, [1, 2, 4]
ZC, XC = 160, 160
TC = 160
HW = 336
Q4, U8, BF, F32, I32, U16, F16 = "float8_e4m3fn_x4", "uint8", "bfloat16", "float32", "int32", "uint16", "float16"
ROW, SCO, SUM = [1, 2], [0, 3], [7, 3]
OWN, FAR = [4, 5, 6, 0], [1, 2, 7, 3]
SPLIT = [[3], [2, 3]]
TURN = [2, 3, 1, 0, 4, 5, 6, 7, 9, 8]
HEAD, ALONE = 5, 3
LC, LATE = 128, [6, 7, 9, 8]
JOINT = [(0, 0), (0, 2), (0, 3), (1, 2), (0, 1), (1, 3), (0, None), (1, 0), (1, 1), (1, None)]
AFTER = [("A", "r", 0, 0), ("A", "r", 0, 1), ("A", "r", 0, 2), ("A", "r", 0, 3), ("A", "r", 1, 0), ("V", "g", 0, 0),
         ("A", "r", 1, 1), ("V", "g", 0, 1), ("A", "r", 1, 2), ("V", "g", 0, 2), ("A", "r", 1, 3), ("A", "g", 0, 3),
         ("V", "g", 1, 0), ("V", "q", 0, 0), ("A", "g", 1, 1), ("V", "g", 1, 2), ("A", "g", 1, 3), ("V", "q", 1, 0)]
ACC = [[0, 1], [0, 2]]

SCRATCH = {}


def _sb(name, n, d):
    SCRATCH[name] = ("sbuf", [128, n], d)


def _pair(name, n):
    _sb(name + "q", n, Q4)
    _sb(name + "s", n, U8)


for _n, _w, _d in [
        ("x0", 1280, BF), ("xs", 1280, BF), ("ut", 512, BF), ("vt", 512, BF), ("et", 2048, BF), ("st", 512, BF),
        ("ones", 512, BF), ("eye", 128, BF), ("ioff", 24, F32), ("uoff", 24, U16), ("pc", 8, I32), ("pm", 8, I32),
        ("pf", 8, F32), ("r16", 336, BF), ("r32", 64, BF), ("cq", 80, BF), ("alt", 2 * C, BF),
        ("wi", 20, F32), ("wu", 80, F32), ("mask", 336, BF), ("keep", C, BF), ("cut", 336, BF), ("cols", C, F32),
        ("half", C, BF), ("tp", C, F32), ("qa", 80, BF), ("qq", 80, BF), ("qs", 80, F32), ("sg", 40 * C, BF),
        ("pos", 128, BF), ("neg", 128, BF),
        ("ft", 5 * 1280, BF), ("m1", C, F16), ("m2", C, F16), ("sti", 512, BF),
        ("un", 1280, BF), ("sn", 1280, BF), ("m3", C, BF), ("m4", C, BF), ("td", 80, F32),
        ("s2", 656, BF), ("one", C, BF), ("ih", 20, I32), ("lh", 20, U16), ("ew", 20, F32), ("ev", 20, BF),
        ("os_", 20, U16), ("of_", 20, U16), ("vw", 656, F32), ("y1", 336, F32),
        ("ki", 20, I32), ("kj", 20, I32), ("do_", 1280, BF), ("dp", 1280, BF), ("df", 1280, BF),
        ("zo", 1280, BF), ("zi", 1280, BF), ("z", 1280, BF), ("hs", 4 * HW, BF), ("hp", 1280, BF),
        ("fr", 2 * C, BF), ("fm", 2 * C, BF), ("fo", C, F32), ("yo", C, F32)]:
    _sb(_n, _w, _d)
for _n, _w in [("u", 128), ("up", 384), ("v", 128), ("w", 512), ("e", 512), ("s", 128), ("f", 5 * C), ("z", C), ("h", C)]:
    _pair("c" + _n, _w)
for _t in range(R + 1):
    _pair("t%d" % _t, C)
for _t in range(R):
    _pair("l%d" % _t, C)
    for _n in ("lo", "la", "li", "lb"):
        _sb("%s%d" % (_n, _t), 20, U16)
SCRATCH["ps"] = ("psum", [128, 4096], F32)

SEMAPHORES = (["cV", "cA", "cT", "cG", "sent", "dx0", "dx1", "du", "dv", "dw", "out", "aQ", "aS"]
              + ["%s%d" % (n, t) for t in range(R) for n in ("aT", "aA", "aB")])


def helper(core, T, topo):
    here = [c for c in T.cores if topo.chip(c) == topo.chip(core)]
    spare = [c for c in topo.cores_of(core) if c not in T.cores and topo.die(c) != topo.die(core)]
    return spare[here.index(core)]


def hand_on(g, core, T, topo):
    for rank, src in enumerate(T.cores):
        for t in range(R):
            dst = T.cores[rank ^ STEP[t]]
            if topo.chip(src) != topo.chip(dst) and helper(src, T, topo) == core:
                rid, pid, _ = topo.addr(dst)
                for sem, ap in (("aQ", T["l%dq" % t][:, TC:C].bitcast(dt.uint8)), ("aS", T["l%ds" % t][:, TC:C])):
                    g.wait_ge(T.sem[sem], len(topo.engines(src, core)))
                    g.remote_dma(ap, ap, T.sem["aT%d" % t], T.sem.sent, pid, rid, topo.mask(core, dst))
                g.wait_ge(T.sem.sent, 2 * len(topo.engines(core, dst)))


def rank_program(g, core, T, topo):
    rank = T.rank_of(core)
    if rank is None:
        return hand_on(g, core, T, topo)
    A = AluOpType
    F = ActivationFunctionType
    queue = {"V": g.vector, "A": g.scalar, "T": g.tensor, "G": g, "S": g.sync}
    own = {"V": "cV", "A": "cA", "T": "cT", "G": "cG"}
    count = {}
    clock = {k: {} for k in queue}
    events = []
    wrote, read = {}, {}

    def view(name, a=0, b=None, s=1, p=None):
        n = SCRATCH[name][1][1]
        b = n if b is None else b
        rows = slice(0, 128) if p is None else slice(p[0], p[1])
        ap = T[name][rows, a:b] if s == 1 else T[name][rows, a:b:s]
        if name == "ps":
            return (ap, [(name, np.arange(a // 512, a // 512 + 1))])
        return (ap, [(name, np.arange(a, b, s))])

    def bank(k, n=C, a=0):
        return view("ps", 512 * k + a, 512 * k + n)

    def by(win, off):
        return (win[0].indirect(off[0]), win[1] + off[1])

    def cast(x, d):
        return (x[0].bitcast(d), x[1])

    def marks(table, name):
        if name not in table:
            n = 8 if name == "ps" else SCRATCH[name][1][1]
            table[name] = {k: np.full(n, -1) for k in list(queue) + ["X"]}
        return table[name]

    def wait(q, sem, val, snap):
        if clock[q].get(sem, 0) < val:
            queue[q].wait_ge(T.sem[sem], int(val))
            clock[q][sem] = val
        for k in snap:
            if clock[q].get(k, 0) < snap[k]:
                clock[q][k] = snap[k]

    def order(q, outs, ins, adds=False):
        need = set()
        for x in ins:
            for name, idx in x[1]:
                for k, m in marks(wrote, name).items():
                    need.update(m[idx].tolist())
                if name == "ps":
                    for k, m in marks(read, name).items():
                        if k != q:
                            need.update(m[idx].tolist())
        for x in outs:
            for name, idx in x[1]:
                for table in (wrote, read):
                    for k, m in marks(table, name).items():
                        if not (adds and k == q):
                            need.update(m[idx].tolist())
        need.discard(-1)
        for e in sorted(need, reverse=True):
            wait(q, events[e][0], events[e][1], events[e][3])

    def note(q, sem, n, outs, ins):
        count[sem] = count.get(sem, 0) + n
        events.append((sem, count[sem], q, dict(clock[q]) if q != "X" else {}))
        for table, xs in ((read, ins), (wrote, outs)):
            for x in xs:
                for name, idx in x[1]:
                    marks(table, name)[q][idx] = len(events) - 1

    def run(q, call, outs, ins, adds=False):
        order(q, outs, ins, adds)
        call().then_inc(T.sem[own[q]], 1)
        note(q, own[q], 1, outs, ins)

    def isview(x):
        return isinstance(x, tuple)

    def copy(out, in_):
        run("V", lambda: g.vector.tensor_copy(out[0], in_[0]), [out], [in_])

    def scatter(win, off, vals):
        run("V", lambda: g.vector.tensor_copy(win[0].indirect(off[0]), vals[0]), [win], [off, vals])

    def tt(out, a, b, op):
        run("V", lambda: g.vector.tensor_tensor(out[0], a[0], b[0], op), [out], [a, b])

    def ts(out, a, s1, op0, s2=None, op1=None):
        ins = [a] + [s for s in (s1, s2) if isview(s)]
        x1, x2 = (s1[0] if isview(s1) else s1), (s2[0] if isview(s2) else s2)
        if op1 is None:
            run("V", lambda: g.vector.tensor_scalar(out[0], a[0], x1, None, op0), [out], ins)
        else:
            run("V", lambda: g.vector.tensor_scalar(out[0], a[0], x1, x2, op0, op1), [out], ins)

    def scan(out, d0, d1, init, op0, op1):
        run("V", lambda: g.vector.tensor_tensor_scan(out[0], d0[0], d1[0], init, op0, op1), [out], [d0, d1])

    def fill(out, c):
        run("V", lambda: g.vector.memset(out[0], c), [out], [])

    def act(out, in_, func, bias=None, scale=None):
        kw = {}
        if bias is not None:
            kw["bias"] = bias[0] if isview(bias) else bias
        if scale is not None:
            kw["scale"] = scale[0] if isview(scale) else scale
        run("A", lambda: g.scalar.activation(out[0], in_[0], func, **kw), [out],
            [in_] + [x for x in (bias, scale) if isview(x)])

    def move(on_vector, out, in_):
        if on_vector:
            copy(out, in_)
        else:
            act(out, in_, F.Copy)

    def pair(name, a=0, b=None):
        return (view(name + "q", a, b), view(name + "s", a, b))

    def quant(p, tile):
        run("V", lambda: g.vector.quantize_mx(p[0][0], p[1][0], tile[0]), [p[0], p[1]], [tile])

    def mm(out, w, x, start=True, stop=True):
        run("T", lambda: g.tensor.matmul_mx(out[0], w[0][0], w[1][0], x[0][0], x[1][0], start, stop),
            [out], [w[0], w[1], x[0], x[1]], adds=not start)

    def iota(out, pattern, base, mult):
        if SCRATCH[out[1][0][0]][2] == I32:
            run("G", lambda: g.iota(out[0], pattern, base, mult), [out], [])
        else:
            run("G", lambda: g.iota(out[0], pattern, base, mult, allow_small_or_imprecise_dtypes=True), [out], [])

    def load(q, sem, jobs):
        for out, src in jobs:
            queue[q].dma_start(out[0], src).then_inc(T.sem[sem], 16)
        note(q, sem, 16 * len(jobs), [j[0] for j in jobs], [])

    def store(q, dst, src):
        order(q, [], [src])
        queue[q].dma_start(dst, src[0]).then_inc(T.sem.out, 16)
        count["out"] = count.get("out", 0) + 16

    def send(peer, sem, jobs, helped=False):
        to, last = (helper(core, T, topo), helper(peer, T, topo)) if helped else (peer, peer)
        rid, pid, _ = topo.addr(to)
        for (dst, src), there in zip(jobs, ("aQ", "aS") if helped else (sem, sem)):
            order("G", [], [src])
            g.remote_dma(dst[0], src[0], T.sem[there], T.sem.sent, pid, rid, topo.mask(core, to))
            count["sent"] = count.get("sent", 0) + len(topo.engines(core, to))
        note("X", sem, len(topo.engines(last, core)) * len(jobs), [j[0] for j in jobs], [])

    XP, ZP, LP = [(0, XC), (XC, C)], [(0, ZC), (ZC, C)], [(LC, C), (0, LC)]
    E = [pair("ce", 128 * b, 128 * b + 128) for b in range(4)]
    W = [pair("cw", 128 * b, 128 * b + 128) for b in range(4)]
    UP = [pair("cup", 128 * k, 128 * k + 128) for k in range(3)]
    p16, p32, p4, run32 = [view("pf", k, k + 1) for k in range(4)]

    load("A", "du", [(view("ut"), T.u[:])])
    for i, (a, b) in enumerate(XP):
        load("S", "dx%d" % i, [(view("x0", 4 * a, 4 * b), T.x[:, 4 * a:4 * b])])
    fill(view("ones"), 1.0)
    iota(view("pc", 0, 1), [[1, 1]], 0, 1)
    iota(view("ioff", 0, 16), [[16, 2], [32, 4], [0, 2]], 0, 0)
    iota(view("ioff", 16, 24), [[16, 8]], 0, 0)
    iota(view("r32"), [[1, 32], [0, 2]], 0, 0)
    iota(view("sti"), [[1, 8], [0, 32], [-1, 2]], 0, 0)
    run("G", lambda: g.affine_select(T.eye[:], T.ones[:, 0:128], [[1, 128]], A.is_equal, 0.0, 0, -1),
        [view("eye")], [view("ones", 0, 128)])
    iota(view("pos"), [[0, 64], [1, 2]], 0, 0)
    iota(view("neg"), [[0, 64], [-1, 2]], 0, 0)
    iota(view("r16"), [[0, 21], [1, 16]], 0, 0)
    for b in range(4):
        act(view("et", 512 * b, 512 * b + 512), view("ones"), F.Copy, None, 0.0)
    ts(view("pm", 0, 1), view("pc", 0, 1), 15, A.bitwise_and)
    ts(view("pm", 1, 2), view("pc", 0, 1), 31, A.bitwise_and)
    ts(view("pm", 2, 3), view("pc", 0, 1), 15, A.bitwise_and, 2, A.logical_shift_right)
    ts(view("pm", 3, 4), view("pc", 0, 1), 5, A.logical_shift_right)
    fill(view("cq"), 8.0)
    copy(view("pf", 0, 4), view("pm", 0, 4))
    copy(view("uoff", 0, 16), view("ioff", 0, 16))
    ts(view("uoff", 16, 24), view("ioff", 16, 24), p4, A.add)
    fill(view("cq", 1, 80, 4), 1.0)
    fill(view("keep"), 1.0)
    for b in TURN:
        ts(view("sg", 4 * C * b + 128 * b, 4 * C * b + 128 * b + 128, 2), view("r32"), p32, A.is_gt, 0.5, A.subtract)
    ts(view("st"), view("sti"), 0.5, A.mult, run32, A.is_equal)
    fill(view("keep", 0, C, 16), 0.0)
    quant(pair("cs"), view("st"))
    for b in range(4):
        act(view("et", 512 * b + b, 512 * b + 512, 4), view("eye"), F.Copy)
    quant(pair("cu"), view("ut"))
    for a, b in ((16, 24), (0, 16)):
        copy(cast(view("cupq", 16 * a, 16 * b), dt.uint32), by(cast(view("cuq"), dt.uint32), view("uoff", a, b)))
        act(view("cups", 16 * a, 16 * b), by(view("cus"), view("uoff", a, b)), F.Copy)

    def prices(name, i):
        a, b = XP[i]
        mm(bank(SCO[i], b - a), UP[2], pair(name, a, b))

    def turn(i):
        a, b = XP[i]
        src, dst = bank(SCO[i], b - a), view("tp", a, b)
        run("V", lambda: g.vector.transpose(dst[0], src[0]), [dst], [src])

    def lots(i):
        a, b = XP[i][0] // 4, XP[i][1] // 4
        return [lambda: ts(view("qa", a, b), view("tp", 4 * a, 4 * b, 4), 0.0, A.is_gt),
                lambda: scan(view("qq", a, b), view("cq", a, b), view("qa", a, b), 1.0, A.min, A.add)]

    quant(pair("t0", 0, XC), view("x0", 0, 4 * XC))
    prices("t0", 0)
    quant(pair("ce", 0, 256), view("et", 0, 1024))
    quant(pair("t0", XC, C), view("x0", 4 * XC, 4 * C))

    for t in range(R):
        mate = rank ^ STEP[t]
        peer = T.cores[mate]
        buys = rank < mate
        mine, theirs = "t%d" % t, "l%d" % t
        lo, la, li, lb = [view("%s%d" % (n, t)) for n in ("lo", "la", "li", "lb")]

        def hand(a, b, helped=False):
            send(peer, "aT%d" % t, [(cast(view(theirs + "q", a, b), dt.uint8), cast(view(mine + "q", a, b), dt.uint8)),
                                    (view(theirs + "s", a, b), view(mine + "s", a, b))], helped)

        turn(0)
        if t == 0:
            quant(pair("ce", 256, 512), view("et", 1024, 2048))
        lots(0)[0]()
        mm(bank(ROW[0]), UP[0], pair(mine))
        prices(mine, 1)
        mm(bank(ROW[1]), UP[1], pair(mine))
        if topo.chip(core) == topo.chip(peer):
            hand(0, C)
        else:
            hand(0, TC)
            hand(TC, C, True)
        if t == 0:
            iota(view("un"), [[0, 1280]], 0, 0)
            iota(view("one"), [[0, C]], -1, 0)
            iota(view("s2", 0, 1), [[0, 1]], 160, 0)
            iota(view("wu"), [[0, 20], [8192, 2], [0, 2]], -4096, 0)
            iota(view("wi"), [[16, 20]], 164, 0)
        for b in range(4):
            mm(bank(OWN[b]), E[b], pair(mine))
        cmp_, loose = (A.is_gt, -0.5) if buys else (A.is_lt, 0.5)

        def signs(b, h, a0, a1):
            s0 = 4 * C * b + 2 * h + 1
            return view("sg", s0 + 4 * a0, s0 + 4 * a1 - 3, 4)

        def flags(b, h, a0, a1):
            f0 = 1280 * (b // 2) + 2 * (b % 2) + h
            return view("ft", f0 + 4 * a0, f0 + 4 * a1 - 3, 4)

        def sign(b, h, a0, a1):
            m = 2 * b + h
            act(signs(b, h, a0, a1), bank(ROW[h], a1, a0), F.Sign, view("tp", 16 * m, 16 * m + 1), -1.0)

        def earlier(b, h, a0, a1, lim):
            m = 2 * b + h
            if a1 > a0:
                ts(flags(b, h, a0, a1), signs(b, h, a0, a1), lim, cmp_, view("qq", 4 * m + 3, 4 * m + 4), A.mult)

        def parts(b):
            a0 = LC if b in LATE else 0
            lo_, hi_ = 32 * b, 32 * b + 32
            if lo_ == a0 or (hi_ != C and lo_ - a0 >= C - hi_):
                return (a0, lo_, 0.0), (lo_, C, loose)
            return (hi_, C, loose), (a0, hi_, 0.0)

        def free(b, h):
            earlier(b, h, *parts(b)[0])

        def direct(b, h):
            m, (a0, a1, lim) = 2 * b + h, parts(b)[0]
            op = [[A.is_gt, A.is_ge], [A.is_lt, A.is_le]][buys][lim != 0.0]
            ts(flags(b, h, a0, a1), bank(ROW[h], a1, a0), view("tp", 16 * m, 16 * m + 1), op,
               view("qs", 4 * m + 3, 4 * m + 4), A.mult)

        def strict(b, h):
            m = 2 * b + h
            act(flags(b, h, 0, LC), signs(b, h, 0, LC), F.Relu, None, view("qs", 4 * m + 3, 4 * m + 4))

        def ties(b):
            d = view("sg", 4 * C * b + 128 * b, 4 * C * b + 128 * b + 128)
            scan(d, view("pos" if buys else "neg"), d, 0.0, A.mult, A.add)

        def tied(b):
            for h in range(2):
                earlier(b, h, *parts(b)[1])

        def total(w, pieces):
            a0, a1 = LP[pieces[-1]][0], LP[pieces[0]][1]
            quant(pair("cf", C * w + a0, C * w + a1), view("ft", 1280 * w + 4 * a0, 1280 * w + 4 * a1))
            for i in pieces:
                a, b = LP[i]
                mm(bank(SUM[i], b - a), pair("cs"), pair("cf", C * w + a, C * w + b), w == TURN[0] // 2, w == TURN[-1] // 2)

        for b in TURN[:HEAD]:
            sign(b, 0, 0, C)
        lots(0)[1]()
        turn(1)
        copy(view("qs", 0, XC // 4), view("qq", 0, XC // 4))
        lots(1)[0]()
        for b in TURN[:ALONE]:
            direct(b, 1)
        lots(1)[1]()
        free(TURN[0], 0)
        for b in TURN[:HEAD]:
            sign(b, 1, *(parts(b)[1][:2] if b in TURN[:ALONE] else (0, C)))
        for b in TURN[1:HEAD]:
            free(b, 0)
        ties(TURN[0])
        for n, b in enumerate(TURN[1:], 1):
            if n == HEAD:
                ts(view("qs", 48, 80), view("qq", 48, 80), 1.0 if buys else -1.0, A.mult)
            if n >= HEAD:
                for h in range(2):
                    sign(b, h, 0, C)
                free(b, 0)
            if n >= ALONE:
                free(b, 1)
            ties(b)
            if n % 2 and n > 1:
                total(TURN[n - 2] // 2, [0] if TURN[n - 2] in LATE else [0, 1])
            tied(TURN[n - 1])
        for b in LATE:
            for h in range(2):
                strict(b, h)
        if t == 0:
            ts(view("mask"), view("r16"), p16, A.is_equal)
        tied(LATE[-1])
        total(LATE[0] // 2, [1])
        total(LATE[-1] // 2, [0])
        total(LATE[-1] // 2, [1])
        for i, (a, b) in enumerate(LP):
            tt(view("m1", a, b), bank(SUM[i], b - a), view("mask", a, b), A.mult)
        for a, b in LP:
            scan(view("m2", a, b), view("keep", a, b), view("m1", a, b), 0.0, A.mult, A.add)
        copy(lo, view("m2", 15, C, 16))
        send(peer, "aA%d" % t, [(la, lo)])

        if t == 0:
            iota(view("cols"), [[1, C]], 0, 0)
            iota(view("vw", 0, 336), [[0, 336]], -16384, 0)
            iota(view("alt"), [[0, C], [1, 2]], 0, 0)
            act(view("cut"), view("mask"), F.Identity, 512.0, -2.0 ** 20)
            act(view("wu", 3, 80, 4), view("wi"), F.Identity, p16)
            act(view("half"), view("one"), F.Copy, None, 0.5)
            act(view("hs", 15, 4 * HW, HW), view("ones", 0, 4), F.Copy, None, 0.0)
        mark = view("one" if t + 1 < R else "half")
        if t + 1 < R:
            ts(view("ih"), view("m2", 15, C, 16), 0.5, A.mult, 0.25, A.add)
        scatter(view("un"), lo, mark)
        for b in range(4):
            mm(bank(FAR[b]), E[b], pair(theirs))
        for b in range(4):
            act(view("do_", C * b, C * b + C), bank(OWN[b]), F.Copy, None, 0.5)
            for i, (a0, a1) in enumerate(XP):
                if b not in ACC[i]:
                    act(view("df", C * b + a0, C * b + a1), bank(OWN[b], a1, a0), F.Copy)
        for b in range(4):
            act(view("dp", C * b, C * b + C), bank(FAR[b]), F.Copy, None, 0.5)

        if t == 0:
            order("S", [], [la])
            load("S", "dw", [(cast(view("cwq"), dt.uint8), T.wc[:]), (view("cws"), T.ws[:])])
        if t == 1:
            order("S", [], [la])
            load("S", "dv", [(view("vt"), T.v[:])])
        scatter(view("un"), la, mark)
        seg = view("m4", 15, C, 16)
        if t + 1 < R:
            copy(view("lh"), view("ih"))
            scan(view("s2", 1, 641), view("un", 0, 1280, 2), view("un", 1, 1280, 2), 160.0, A.add, A.add)
            ts(view("ew"), view("ih"), -2.0, A.mult, 1.0, A.add)
            tt(view("m3"), by(view("s2"), view("lh")), view("mask", 0, C), A.mult)
            tt(view("ev"), view("ew"), view("m2", 15, C, 16), A.add)
            scan(view("m4"), view("keep"), view("m3"), 0.0, A.mult, A.add)
            tt(seg, seg, view("ev"), A.subtract)
        else:
            scan(view("sn"), view("un"), view("un"), 160.0, A.add, A.add)
            tt(view("m3"), by(view("sn"), lo), view("mask", 0, C), A.mult)
            act(view("fr", 0, 2 * C, 2), by(view("sn"), lo), F.Copy)
            act(view("fr", 1, 2 * C, 2), view("fr", 0, 2 * C, 2), F.Relu, -160.5 * 4096, -4096.0)
            scan(view("m4"), view("keep"), view("m3"), 0.0, A.mult, A.add)
        ts(view("m4", 11, C, 16), seg, 160.5, A.add, -4096.0, A.mult)
        ts(view("of_"), seg, -161.0, A.max, 176.0, A.add)
        scan(view("td"), view("m4", 3, C, 4), view("wu"), 0.0, A.max, A.min)
        ts(view("os_"), view("td", 3, 80, 4), 160.0, A.add)
        scatter(view("vw"), view("os_"), view("cols"))
        scan(view("y1", 0, 324), view("cut", 0, 324), view("vw", 0, 324), 0.0, A.add, A.max)
        tt(view("ki"), view("y1", 15, C, 16), view("y1", 18, C + 3, 16), A.max)
        ts(view("kj"), view("ki"), 511, A.bitwise_and)
        copy(li, view("kj"))
        send(peer, "aB%d" % t, [(lb, li)])

        if t + 1 < R:
            iota(view("un"), [[0, 1280]], 0, 0)
            iota(view("vw", 0, 336), [[0, 336]], -16384, 0)
        for b in range(4):
            for a0, a1 in ([(0, C)] if b < 2 else ZP):
                if b in SPLIT[a0 > 0]:
                    out = view("zi", 2 * C * (b - 2) + 2 * a0, 2 * C * (b - 2) + 2 * a1, 2)
                else:
                    out = view("zo", C * b + a0, C * b + a1)
                move(b >= 2, out, by(view("do_", C * b, C * b + C), view("li%d" % t, a0 // 16, a1 // 16)))
        if t + 1 == R:
            scan(view("fm"), view("alt"), view("fr"), 0.0, A.mult, A.subtract)

        def far(b, a0, a1):
            return by(view("dp", C * b, C * b + C), view("lb%d" % t, a0 // 16, a1 // 16))

        for i, (a0, a1) in enumerate(ZP):
            for b in SPLIT[i]:
                o = 2 * C * (b - 2)
                act(view("zi", o + 2 * a0 + 1, o + 2 * a1, 2), far(b, a0, a1), F.Copy)
        for i, b in JOINT:
            a0, a1 = ZP[i]
            if b is None:
                quant(pair("cz", a0, a1), view("z", 4 * a0, 4 * a1))
            elif b in SPLIT[i]:
                o = 2 * C * (b - 2)
                scan(view("z", 4 * a0 + b - 2, 4 * a1, 2), view("alt", 2 * a0, 2 * a1),
                     view("zi", o + 2 * a0, o + 2 * a1), 0.0, A.mult, A.add)
            else:
                tt(view("z", 4 * a0 + b, 4 * a1, 4), far(b, a0, a1), view("zo", C * b + a0, C * b + a1), A.add)
        for i, (a0, a1) in enumerate(ZP):
            for b in range(4):
                mm(bank(4 * i + b, a1 - a0), W[b], pair("cz", a0, a1))
        if t == 1:
            quant(pair("cv"), view("vt"))
        if t + 1 == R:
            ts(view("fo"), view("fm", 1, 2 * C, 2), 159.0, A.add, -1.0, A.max)
            for k in range(8):
                store("S", T.ol[k:k + 1, :], view("fo", 0, C, 1, (16 * k, 16 * k + 1)))

        for q, what, i, b in AFTER:
            if what == "r":
                a0, a1 = ZP[i]
                out = view("hs", HW * b + 16 + a0, HW * b + 16 + a1)
                if q == "V":
                    ts(out, bank(4 * i + b, a1 - a0), 0.0, A.max, 0.03125, A.mult)
                else:
                    act(out, bank(4 * i + b, a1 - a0), F.Relu, None, 0.03125)
            a0, a1 = XP[i]
            if what == "g":
                move(q == "V", view("hp", 4 * a0 + b, 4 * a1, 4),
                     by(view("hs", HW * b, HW * b + HW), view("of_", a0 // 16, a1 // 16)))
            if what == "q":
                quant(pair("ch", a0, a1), view("hp", 4 * a0, 4 * a1))
        for i, (a0, a1) in enumerate(XP):
            for b in ACC[i]:
                mm(bank(4 * i + b, a1 - a0), E[b], pair(mine, a0, a1), True, False)
        nxt = "t%d" % (t + 1)
        for i, (a0, a1) in enumerate(XP):
            for b in range(4):
                mm(bank(4 * i + b, a1 - a0), E[b], pair("ch", a0, a1), b not in ACC[i], True)
                out = view("xs", 4 * a0 + b, 4 * a1, 4)
                if b in ACC[i]:
                    act(out, bank(4 * i + b, a1 - a0), F.Copy)
                else:
                    tt(out, bank(4 * i + b, a1 - a0), view("df", C * b + a0, C * b + a1), A.add)
            if i and t + 1 < R:
                prices(nxt, 0)
            elif i:
                mm(bank(0, XC), pair("cv"), pair(nxt, 0, XC))
            quant(pair(nxt, a0, a1), view("xs", 4 * a0, 4 * a1))

    last = "t%d" % R
    mm(bank(1, C - XC), pair("cv"), pair(last, XC, C))
    for i, (a0, a1) in enumerate(XP):
        store("S", T.oc[:, 4 * a0:4 * a1], cast(view(last + "q", a0, a1), dt.uint8))
    act(view("yo", 0, XC), bank(0, XC), F.Copy)
    store("A", T.y[:, 0:XC], view("yo", 0, XC))
    copy(view("yo", XC, C), bank(1, C - XC))
    for k in range(4):
        store("A", T.osc[4 * k:4 * k + 4, :], view(last + "s", 0, C, 1, (32 * k, 32 * k + 4)))
    store("S", T.y[:, XC:C], view("yo", XC, C))
    g.sync.wait_ge(T.sem.out, count["out"])
    g.wait_ge(T.sem.sent, count["sent"])
    for sem in ("cV", "cA", "cT", "cG"):
        g.wait_ge(T.sem[sem], count[sem])
